import numpy as np
import ml_dtypes


def mxq(x, axis, fmt="e4m3"):
    dtype, down = {"e4m3": (ml_dtypes.float8_e4m3fn, 7), "e5m2": (ml_dtypes.float8_e5m2, 14)}[fmt]
    v = np.moveaxis(np.asarray(x, np.float32).astype(ml_dtypes.bfloat16).astype(np.float64), axis, -1)
    blocks = v.reshape(v.shape[:-1] + (-1, 32))
    amax = np.abs(blocks).max(-1, keepdims=True)
    byte = np.maximum(np.where(amax > 0, np.frexp(amax)[1] - 1 + 127, 0) - down, 1)
    scale = np.exp2(byte - 127.0)
    codes = (blocks / scale).astype(np.float32).astype(dtype).astype(np.float64)
    return np.moveaxis((codes * scale).reshape(v.shape), -1, axis)


WIDE = False


def mx_kscale(k):
    if not WIDE:
        return np.ones(k)
    levels = np.array([10, -10, 5, -5, 0])
    if k % 512:
        return np.exp2(np.random.permutation(np.resize(levels, k // 32))).repeat(32)
    a = np.empty((k // 512, 16))
    for p in range(k // 512):
        a[p, :8] = np.random.permutation(np.resize(levels, 8))
        for g in range(8):
            far = levels[np.abs(levels - a[p, g]) >= 10]
            a[p, g + 8] = far[np.random.randint(len(far))]
    return np.exp2(a.ravel()).repeat(32)


def f64(x):
    return np.asarray(x).astype(np.float64)


def striped(idx):
    return np.tile(idx.reshape(-1, 16).T, (8, 1)).astype(np.uint16)


def unstriped(offs):
    return offs[:16].T.reshape(-1).astype(np.int64)


def pack_weight(w):
    k, n = w.shape
    w = f64(np.asarray(w, np.float32).astype(ml_dtypes.bfloat16)).reshape(k // 32, 32, n)
    amax = np.abs(w).max(1)
    byte = np.clip(np.where(amax > 0, np.frexp(amax)[1] - 1 + 127 - 7, 1), 1, 254)
    scaled = (w * np.exp2(127.0 - byte)[:, None, :]).reshape(k, n).astype(np.float32)
    words = np.ascontiguousarray(scaled.reshape(k // 512, 128, 4, n).transpose(0, 1, 3, 2)).astype(ml_dtypes.float8_e4m3fn).view(np.uint8)
    return words, np.ascontiguousarray(byte.astype(np.uint8).reshape(k // 512, 16, n))


def unpack_weight(words, scales):
    g, p, n, _ = words.shape
    vals = np.ascontiguousarray(words).view(ml_dtypes.float8_e4m3fn).astype(np.float64) * np.repeat(np.exp2(scales.astype(np.float64) - 127.0), 8, axis=1)[..., None]
    return vals.transpose(0, 1, 3, 2).reshape(g * 512, n)


def gelu(v):
    return 0.5 * v * (1.0 + np.tanh(np.sqrt(2.0 / np.pi) * (v + 0.044715 * v**3)))


K, T, S, V, H, N = 512, 1024, 512, 256, 512, 128


def setup_inputs():
    n = np.random.standard_normal
    s = mx_kscale(K)[:, None]
    u = mx_kscale(H)
    near = np.random.permutation(S)
    packed_xT = pack_weight(n((K, T)) * s)
    return {
        "x_words": packed_xT[0],
        "x_scales": packed_xT[1],
        "w1": (n((K, H)) / np.sqrt(2 * K) / s * u).astype(np.float32),
        "w2": (n((K, H)) / np.sqrt(2 * K) / s * u).astype(np.float32),
        "w3": (n((H, N)) / np.sqrt(2 * H) / u[:, None]).astype(np.float32),
        "w4": (n((H, N)) / np.sqrt(2 * H) / u[:, None]).astype(np.float32),
        "offs": striped(np.random.permutation(T)[:S]),
        "right": striped(np.random.permutation(T)[:S]),
        "up1": striped(near[:V]),
        "up2": striped(near[V:]),
    }


def reference(x_words, x_scales, w1, w2, w3, w4, offs, right, up1, up2):
    xq = unpack_weight(x_words, x_scales)[:, unstriped(offs)]
    x_right = unpack_weight(x_words, x_scales)[:, unstriped(right)]
    h = gelu(mxq(f64(w1), 0, "e4m3").T @ xq + mxq(f64(w2), 0, "e4m3").T @ x_right)
    a = h[:, unstriped(up1)]
    ee = h[:, unstriped(up2)]
    return gelu(mxq(f64(w3), 0, "e4m3").T @ mxq(a, 0, "e4m3") + mxq(f64(w4), 0, "e4m3").T @ mxq(ee, 0, "e4m3"))

@@ -1,0 +1,162 @@
+from contextlib import ExitStack
+
+import concourse.mybir as mybir
+
+K, T, S, V, H, N = 512, 1024, 512, 256, 512, 128
+FLOPS = 2 * (2 * K * H * S + 2 * H * N * V)
+
+F32 = mybir.dt.float32
+BF16 = mybir.dt.bfloat16
+I32 = mybir.dt.int32
+U32 = mybir.dt.uint32
+U16 = mybir.dt.uint16
+U8 = mybir.dt.uint8
+FP8X4 = mybir.dt.float8_e4m3fn_x4
+GELU = mybir.ActivationFunctionType.Gelu_apprx_tanh
+
+P = 128
+PACK = 4
+HALF = P // 2
+
+
+def tile_picked_yrecnn_gelu_p_kernel(
+    tc, x_words, x_scales, w1, w2, w3, w4, offs, right, up1, up2, out
+):
+    nc = tc.nc
+    with ExitStack() as ctx:
+        lists = ctx.enter_context(tc.tile_pool(name="lists", bufs=1))
+        sb = ctx.enter_context(tc.tile_pool(name="sb", bufs=1))
+        psum = ctx.enter_context(tc.psum_pool(name="psum", bufs=1))
+
+        def tile(name, shape, dtype):
+            return sb.tile(shape, dtype, name=name, align_bytes=64)
+
+        def load_list(name, src):
+            dst = lists.tile(list(src.shape), U16, name=name)
+            nc.sync.dma_start(dst[:], src)
+            return dst
+
+        def load_rows(name, w, cols):
+            dst = tile(name, [P, PACK, cols.stop - cols.start], F32)
+            nc.sync.dma_start(out=dst[:], in_=w.rearrange("(p j) c -> p j c", j=PACK)[:, :, cols])
+            return dst
+
+        def quantize(codes, scales, grouped):
+            nc.vector.quantize_mx(out=codes.bitcast(FP8X4), scales=scales, in_=grouped)
+
+        def mx(acc, w_codes, w_scales, x_codes, x_sc, first):
+            nc.tensor.matmul_mx(
+                out=acc,
+                lhsT=w_codes.bitcast(FP8X4),
+                lhsT_scale=w_scales,
+                rhs=x_codes.bitcast(FP8X4),
+                rhs_scale=x_sc,
+                start=first,
+                stop=not first,
+            )
+
+        offs_sb = load_list("offs_sb", offs)
+        right_sb = load_list("right_sb", right)
+        scale_table = tile("scale_table", [P, T], U8)
+        for q in range(4):
+            rows = x_scales[0, 4 * q : 4 * q + 4, :].bitcast(I32)
+            nc.scalar.dma_start(
+                out=scale_table[32 * q : 32 * q + 32, :].bitcast(I32),
+                in_=rows.unsqueeze(0).to_broadcast([8, 4, T // 4]),
+            )
+        w1_raw = load_rows("w1_raw", w1, slice(0, H))
+        word_table = tile("word_table", [P, T], I32)
+        nc.sync.dma_start(out=word_table[:], in_=x_words[0].rearrange("p n r -> p (n r)").bitcast(I32))
+        w2_raw = [load_rows("w2_raw%d" % u, w2, slice(u * H // 2, (u + 1) * H // 2)) for u in range(2)]
+        up1_sb = load_list("up1_sb", up1)
+        up2_sb = load_list("up2_sb", up2)
+        w3_raw = load_rows("w3_raw", w3, slice(0, N))
+        w4_raw = load_rows("w4_raw", w4, slice(0, N))
+
+        warm_in = tile("warm_in", [P, 8], F32)
+        warm_out = tile("warm_out", [P, 8], F32)
+        nc.gpsimd.memset(warm_in[:], 0.0)
+        nc.scalar.activation(warm_out[:], warm_in[:], GELU)
+
+        picked = []
+        for name, lst in (("left", offs_sb), ("right", right_sb)):
+            sc = tile(name + "_scales", [P, S], U8)
+            nc.vector.tensor_copy(sc[:], scale_table[:].indirect(lst[:]))
+            picked.append([None, sc])
+        for n, (name, lst) in enumerate((("left", offs_sb), ("right", right_sb))):
+            words = tile(name + "_words", [P, S], U32)
+            nc.vector.tensor_copy(words[:], word_table[:].bitcast(U32).indirect(lst[:]))
+            picked[n][0] = words
+
+        w1_grouped = tile("w1_grouped", [P, PACK, P, PACK], BF16)
+        nc.scalar.copy(
+            w1_grouped[:].rearrange("p t m j -> p m j t"),
+            w1_raw[:].rearrange("p j (m t) -> p m j t", t=PACK),
+        )
+        w1_codes = [tile("w1_codes%d" % t, [P, P], U32) for t in range(PACK)]
+        w1_scales = [tile("w1_scales%d" % t, [P, P], U8) for t in range(PACK)]
+        acc = [psum.tile([P, S], F32, name="acc%d" % t) for t in range(PACK)]
+        for t in range(PACK):
+            quantize(w1_codes[t][:], w1_scales[t][:], w1_grouped[:, t].rearrange("p m j -> p (m j)"))
+            mx(acc[t][:], w1_codes[t][:], w1_scales[t][:], picked[0][0][:], picked[0][1][:], True)
+
+        w2_lo = tile("w2_lo", [P, PACK, HALF, PACK], BF16)
+        nc.scalar.copy(
+            w2_lo[:].rearrange("p t m j -> p m j t"),
+            w2_raw[0][:].rearrange("p j (m t) -> p m j t", t=PACK),
+        )
+        w2_hi = [tile("w2_hi%d" % u, [P, 2, HALF, PACK], BF16) for u in range(2)]
+        w2_hi_src = w2_raw[1][:].rearrange("p j (m t) -> p m j t", t=PACK)
+        nc.vector.tensor_copy(w2_hi[0][:].rearrange("p t m j -> p m j t"), w2_hi_src[:, :, :, 0:2])
+        nc.scalar.copy(w2_hi[1][:].rearrange("p t m j -> p m j t"), w2_hi_src[:, :, :, 2:4])
+        w2_codes = [tile("w2_codes%d" % t, [P, P], U32) for t in range(PACK)]
+        w2_scales = [tile("w2_scales%d" % t, [P, P], U8) for t in range(PACK)]
+        h = [tile("h%d" % t, [P, S], F32) for t in range(PACK)]
+        for t in range(PACK):
+            quantize(w2_codes[t][:, :HALF], w2_scales[t][:, :HALF], w2_lo[:, t].rearrange("p m j -> p (m j)"))
+            quantize(w2_codes[t][:, HALF:], w2_scales[t][:, HALF:], w2_hi[t // 2][:, t % 2].rearrange("p m j -> p (m j)"))
+            mx(acc[t][:], w2_codes[t][:], w2_scales[t][:], picked[1][0][:], picked[1][1][:], False)
+            nc.scalar.activation(h[t][:], acc[t][:], GELU)
+
+        w34_grouped = tile("w34_grouped", [P, 2, N, PACK], BF16)
+        for u, raw in enumerate((w3_raw, w4_raw)):
+            nc.vector.tensor_copy(
+                w34_grouped[:, u].rearrange("p (c i) j -> p c j i", i=4),
+                raw[:].rearrange("p j (c i) -> p c j i", i=4),
+            )
+        w34_codes = tile("w34_codes", [P, 2 * N], U32)
+        w34_scales = tile("w34_scales", [P, 2 * N], U8)
+        quantize(w34_codes[:], w34_scales[:], w34_grouped[:].rearrange("p u c j -> p (u c j)"))
+
+        a_grouped = tile("a_grouped", [P, V, PACK], BF16)
+        e_grouped = tile("e_grouped", [P, V, PACK], BF16)
+        a_pair = [tile("a_pair%d" % u, [P, 2, V], BF16) for u in range(2)]
+        e_pair = tile("e_pair", [P, 2, V], BF16)
+
+        def weave(grouped, pair, u):
+            nc.scalar.copy(
+                grouped[:, :, 2 * u : 2 * u + 2].rearrange("p (c i) t -> p c t i", i=4),
+                pair[:].rearrange("p t (c i) -> p c t i", i=4),
+            )
+
+        for t in range(PACK):
+            nc.vector.tensor_copy(a_pair[t // 2][:, t % 2], h[t][:].indirect(up1_sb[:]))
+            if t % 2:
+                weave(a_grouped, a_pair[t // 2], t // 2)
+            if t < 2:
+                nc.vector.tensor_copy(e_pair[:, t], h[t][:].indirect(up2_sb[:]))
+            else:
+                nc.vector.tensor_copy(e_grouped[:, :, t], h[t][:].indirect(up2_sb[:]))
+            if t == 1:
+                weave(e_grouped, e_pair, 0)
+
+        acc_out = psum.tile([N, V], F32, name="acc_out")
+        for u, grouped in enumerate((a_grouped, e_grouped)):
+            codes = tile("child_codes%d" % u, [P, V], U32)
+            scales = tile("child_scales%d" % u, [P, V], U8)
+            quantize(codes[:], scales[:], grouped[:].rearrange("p v t -> p (v t)"))
+            cols = slice(u * N, (u + 1) * N)
+            mx(acc_out[:], w34_codes[:, cols], w34_scales[:, cols], codes[:], scales[:], u == 0)
+        result = tile("result", [N, V], F32)
+        nc.scalar.activation(result[:], acc_out[:], GELU)
+        nc.sync.dma_start(out=out, in_=result[:])

@@ -17,6 +17,7 @@ GELU = mybir.ActivationFunctionType.Gelu_apprx_tanh
 P = 128
 PACK = 4
 HALF = P // 2
+H_BYTES = 4 * S
 
 
 def tile_picked_yrecnn_gelu_p_kernel(
@@ -26,10 +27,11 @@ def tile_picked_yrecnn_gelu_p_kernel(
     with ExitStack() as ctx:
         lists = ctx.enter_context(tc.tile_pool(name="lists", bufs=1))
         sb = ctx.enter_context(tc.tile_pool(name="sb", bufs=1))
+        reused = ctx.enter_context(tc.tile_pool(name="reused", bufs=1))
         psum = ctx.enter_context(tc.psum_pool(name="psum", bufs=1))
 
-        def tile(name, shape, dtype):
-            return sb.tile(shape, dtype, name=name, align_bytes=64)
+        def tile(name, shape, dtype, tag=""):
+            return sb.tile(shape, dtype, name=name, tag=tag or name, align_bytes=64)
 
         def load_list(name, src):
             dst = lists.tile(list(src.shape), U16, name=name)
@@ -56,107 +58,143 @@ def tile_picked_yrecnn_gelu_p_kernel(
             )
 
         offs_sb = load_list("offs_sb", offs)
-        right_sb = load_list("right_sb", right)
-        scale_table = tile("scale_table", [P, T], U8)
-        for q in range(4):
-            rows = x_scales[0, 4 * q : 4 * q + 4, :].bitcast(I32)
-            nc.scalar.dma_start(
-                out=scale_table[32 * q : 32 * q + 32, :].bitcast(I32),
-                in_=rows.unsqueeze(0).to_broadcast([8, 4, T // 4]),
-            )
-        w1_raw = load_rows("w1_raw", w1, slice(0, H))
         word_table = tile("word_table", [P, T], I32)
         nc.sync.dma_start(out=word_table[:], in_=x_words[0].rearrange("p n r -> p (n r)").bitcast(I32))
+        right_sb = load_list("right_sb", right)
+        scale_table = tile("scale_table", [P, T], U8)
+        nc.vector.memset(scale_table[:].bitcast(I32), 0)
+        for q in range(4):
+            nc.sync.dma_start(
+                out=scale_table[32 * q : 32 * q + 4, :].bitcast(I32),
+                in_=x_scales[0, 4 * q : 4 * q + 4, :].bitcast(I32),
+            )
+        w1_raw = [load_rows("w1_raw%d" % u, w1, slice(u * H // 2, (u + 1) * H // 2)) for u in range(2)]
         w2_raw = [load_rows("w2_raw%d" % u, w2, slice(u * H // 2, (u + 1) * H // 2)) for u in range(2)]
+        w3_raw = reused.tile([P, PACK * N + 64], F32, name="w3_raw", align_bytes=64, offset=2 * H_BYTES - 128)
+        w4_raw = reused.tile([P, PACK * N], F32, name="w4_raw", align_bytes=64, offset=7 * H_BYTES // 2)
+        w34_raw = [raw[:, : PACK * N].rearrange("p (j c) -> p j c", j=PACK) for raw in (w3_raw, w4_raw)]
+        for raw, w in zip(w34_raw, (w3, w4)):
+            nc.sync.dma_start(out=raw, in_=w.rearrange("(p j) c -> p j c", j=PACK))
         up1_sb = load_list("up1_sb", up1)
         up2_sb = load_list("up2_sb", up2)
-        w3_raw = load_rows("w3_raw", w3, slice(0, N))
-        w4_raw = load_rows("w4_raw", w4, slice(0, N))
 
         warm_in = tile("warm_in", [P, 8], F32)
         warm_out = tile("warm_out", [P, 8], F32)
         nc.gpsimd.memset(warm_in[:], 0.0)
         nc.scalar.activation(warm_out[:], warm_in[:], GELU)
 
-        picked = []
-        for name, lst in (("left", offs_sb), ("right", right_sb)):
-            sc = tile(name + "_scales", [P, S], U8)
-            nc.vector.tensor_copy(sc[:], scale_table[:].indirect(lst[:]))
-            picked.append([None, sc])
-        for n, (name, lst) in enumerate((("left", offs_sb), ("right", right_sb))):
-            words = tile(name + "_words", [P, S], U32)
+        def pick_words(name, lst):
+            words = tile(name, [P, S], U32)
             nc.vector.tensor_copy(words[:], word_table[:].bitcast(U32).indirect(lst[:]))
-            picked[n][0] = words
+            return words
 
-        w1_grouped = tile("w1_grouped", [P, PACK, P, PACK], BF16)
-        nc.scalar.copy(
-            w1_grouped[:].rearrange("p t m j -> p m j t"),
-            w1_raw[:].rearrange("p j (m t) -> p m j t", t=PACK),
-        )
-        w1_codes = [tile("w1_codes%d" % t, [P, P], U32) for t in range(PACK)]
-        w1_scales = [tile("w1_scales%d" % t, [P, P], U8) for t in range(PACK)]
-        acc = [psum.tile([P, S], F32, name="acc%d" % t) for t in range(PACK)]
-        for t in range(PACK):
-            quantize(w1_codes[t][:], w1_scales[t][:], w1_grouped[:, t].rearrange("p m j -> p (m j)"))
-            mx(acc[t][:], w1_codes[t][:], w1_scales[t][:], picked[0][0][:], picked[0][1][:], True)
+        def pick_scales(name, lst, tag=""):
+            sc = tile(name, [P, S], U8, tag=tag)
+            nc.vector.tensor_copy(sc[:], scale_table[:].indirect(lst[:]))
+            return sc
 
-        w2_lo = tile("w2_lo", [P, PACK, HALF, PACK], BF16)
-        nc.scalar.copy(
-            w2_lo[:].rearrange("p t m j -> p m j t"),
-            w2_raw[0][:].rearrange("p j (m t) -> p m j t", t=PACK),
-        )
-        w2_hi = [tile("w2_hi%d" % u, [P, 2, HALF, PACK], BF16) for u in range(2)]
-        w2_hi_src = w2_raw[1][:].rearrange("p j (m t) -> p m j t", t=PACK)
-        nc.vector.tensor_copy(w2_hi[0][:].rearrange("p t m j -> p m j t"), w2_hi_src[:, :, :, 0:2])
-        nc.scalar.copy(w2_hi[1][:].rearrange("p t m j -> p m j t"), w2_hi_src[:, :, :, 2:4])
-        w2_codes = [tile("w2_codes%d" % t, [P, P], U32) for t in range(PACK)]
-        w2_scales = [tile("w2_scales%d" % t, [P, P], U8) for t in range(PACK)]
-        h = [tile("h%d" % t, [P, S], F32) for t in range(PACK)]
-        for t in range(PACK):
-            quantize(w2_codes[t][:, :HALF], w2_scales[t][:, :HALF], w2_lo[:, t].rearrange("p m j -> p (m j)"))
-            quantize(w2_codes[t][:, HALF:], w2_scales[t][:, HALF:], w2_hi[t // 2][:, t % 2].rearrange("p m j -> p (m j)"))
-            mx(acc[t][:], w2_codes[t][:], w2_scales[t][:], picked[1][0][:], picked[1][1][:], False)
-            nc.scalar.activation(h[t][:], acc[t][:], GELU)
+        picked = [[pick_words("left_words", offs_sb), pick_scales("left_scales", offs_sb)]]
+        right_words = pick_words("right_words", right_sb)
+
+        grouped = [tile("grouped%d" % u, [P, PACK, P, PACK], BF16) for u in range(2)]
+
+        def group(engine_copy, raw, u, half, planes):
+            engine_copy(
+                grouped[u][:, planes, half * HALF : (half + 1) * HALF, :].rearrange("p t m j -> p m j t"),
+                raw[:].rearrange("p j (m t) -> p m j t", t=PACK)[:, :, :, planes],
+            )
+
+        w_codes = {}
+        w_scales = {}
+
+        def quantize_weights(name, src, keys, tag=""):
+            codes = tile(name + "_codes", [P, len(keys) * P], U32, tag=tag)
+            scales = tile(name + "_scales", [P, len(keys) * P], U8)
+            quantize(codes[:], scales[:], src)
+            for n, key in enumerate(keys):
+                w_codes[key] = codes[:, n * P : (n + 1) * P]
+                w_scales[key] = scales[:, n * P : (n + 1) * P]
+
+        spans = [[slice(0, S // 2), slice(S // 2, S)]] + [[slice(0, S)]] * (PACK - 1)
+        acc = [
+            [psum.tile([P, cols.stop - cols.start], F32, name="acc%d_%d" % (t, n)) for n, cols in enumerate(spans[t])]
+            for t in range(PACK)
+        ]
+        h = []
+
+        def first_level(t, u):
+            for n, cols in enumerate(spans[t]):
+                mx(acc[t][n][:], w_codes[t, u], w_scales[t, u], picked[u][0][:, cols], picked[u][1][:, cols], u == 0)
+
+        def activate(t):
+            h.append(reused.tile([P, S], F32, name="h%d" % t, align_bytes=64, offset=t * H_BYTES))
+            for n, cols in enumerate(spans[t]):
+                nc.scalar.activation(h[t][:, cols], acc[t][n][:], GELU)
+
+        group(nc.scalar.copy, w1_raw[0], 0, 0, slice(0, 4))
+        group(nc.scalar.copy, w1_raw[1], 0, 1, slice(0, 4))
+        quantize_weights("w1_first", grouped[0][:, :2].rearrange("p t m j -> p (t m j)"), [(0, 0), (1, 0)])
+        first_level(0, 0)
+        first_level(1, 0)
+        picked.append([right_words, pick_scales("right_scales", right_sb, tag="w1_raw1")])
+        group(nc.scalar.copy, w2_raw[0], 1, 0, slice(0, 4))
+        group(nc.scalar.copy, w2_raw[1], 1, 1, slice(0, 2))
+        group(nc.scalar.copy, w2_raw[1], 1, 1, slice(2, 4))
+        quantize_weights("w2_first", grouped[1][:, 0].rearrange("p m j -> p (m j)"), [(0, 1)])
+        first_level(0, 1)
+        quantize_weights("w2_second", grouped[1][:, 1].rearrange("p m j -> p (m j)"), [(1, 1)])
+        first_level(1, 1)
+        quantize_weights("w1_rest", grouped[0][:, 2:].rearrange("p t m j -> p (t m j)"), [(2, 0), (3, 0)], tag="w2_raw1")
+        quantize_weights("w2_rest", grouped[1][:, 2:].rearrange("p t m j -> p (t m j)"), [(2, 1), (3, 1)])
+        for t in range(2, PACK):
+            first_level(t, 0)
+            first_level(t, 1)
 
         w34_grouped = tile("w34_grouped", [P, 2, N, PACK], BF16)
-        for u, raw in enumerate((w3_raw, w4_raw)):
-            nc.vector.tensor_copy(
-                w34_grouped[:, u].rearrange("p (c i) j -> p c j i", i=4),
-                raw[:].rearrange("p j (c i) -> p c j i", i=4),
-            )
-        w34_codes = tile("w34_codes", [P, 2 * N], U32)
-        w34_scales = tile("w34_scales", [P, 2 * N], U8)
-        quantize(w34_codes[:], w34_scales[:], w34_grouped[:].rearrange("p u c j -> p (u c j)"))
 
-        a_grouped = tile("a_grouped", [P, V, PACK], BF16)
-        e_grouped = tile("e_grouped", [P, V, PACK], BF16)
-        a_pair = [tile("a_pair%d" % u, [P, 2, V], BF16) for u in range(2)]
-        e_pair = tile("e_pair", [P, 2, V], BF16)
-
-        def weave(grouped, pair, u):
+        def group_second(u):
             nc.scalar.copy(
-                grouped[:, :, 2 * u : 2 * u + 2].rearrange("p (c i) t -> p c t i", i=4),
-                pair[:].rearrange("p t (c i) -> p c t i", i=4),
+                w34_grouped[:, u].rearrange("p (c i) j -> p c j i", i=4),
+                w34_raw[u].rearrange("p j (c i) -> p c j i", i=4),
             )
 
-        for t in range(PACK):
-            nc.vector.tensor_copy(a_pair[t // 2][:, t % 2], h[t][:].indirect(up1_sb[:]))
-            if t % 2:
-                weave(a_grouped, a_pair[t // 2], t // 2)
-            if t < 2:
-                nc.vector.tensor_copy(e_pair[:, t], h[t][:].indirect(up2_sb[:]))
-            else:
-                nc.vector.tensor_copy(e_grouped[:, :, t], h[t][:].indirect(up2_sb[:]))
-            if t == 1:
-                weave(e_grouped, e_pair, 0)
+        activate(0)
+        group_second(0)
+        activate(1)
+        activate(2)
+        group_second(1)
+        activate(3)
+        quantize_weights("w34", w34_grouped[:].rearrange("p u c j -> p (u c j)"), ["w3", "w4"])
 
-        acc_out = psum.tile([N, V], F32, name="acc_out")
-        for u, grouped in enumerate((a_grouped, e_grouped)):
-            codes = tile("child_codes%d" % u, [P, V], U32)
-            scales = tile("child_scales%d" % u, [P, V], U8)
-            quantize(codes[:], scales[:], grouped[:].rearrange("p v t -> p (v t)"))
-            cols = slice(u * N, (u + 1) * N)
-            mx(acc_out[:], w34_codes[:, cols], w34_scales[:, cols], codes[:], scales[:], u == 0)
-        result = tile("result", [N, V], F32)
-        nc.scalar.activation(result[:], acc_out[:], GELU)
-        nc.sync.dma_start(out=out, in_=result[:])
+        a_planes = tile("a_planes", [P, PACK, V], BF16, tag="grouped1")
+        e_planes = tile("e_planes", [P, 2, V], BF16)
+        e_both = reused.tile([P, 2, P, PACK], BF16, name="e_both", align_bytes=64, offset=4 * H_BYTES)
+        for t in range(2):
+            nc.vector.tensor_copy(a_planes[:, t], h[t][:].indirect(up1_sb[:]))
+            nc.vector.tensor_copy(e_planes[:, t], h[t][:].indirect(up2_sb[:]))
+        nc.scalar.copy(
+            e_both[:, :, :, 0:2].rearrange("p s (c i) t -> p (s c) t i", i=4),
+            e_planes[:].rearrange("p t (c i) -> p c t i", i=4),
+        )
+        for t in range(2, PACK):
+            nc.vector.tensor_copy(a_planes[:, t], h[t][:].indirect(up1_sb[:]))
+        a_both = tile("a_both", [P, 2, P, PACK], BF16)
+        for s in range(2):
+            nc.scalar.copy(
+                a_both[:, s].rearrange("p (c i) t -> p c t i", i=4),
+                a_planes[:, :, s * P : (s + 1) * P].rearrange("p t (c i) -> p c t i", i=4),
+            )
+        nc.vector.tensor_copy(e_both[:, :, :, 2].rearrange("p s v -> p (s v)"), h[2][:].indirect(up2_sb[:]))
+        for s in range(2):
+            nc.vector.tensor_copy(e_both[:, s, :, 3], h[3][:].indirect(up2_sb[:, 8 * s : 8 * s + 8]))
+
+        for s in range(2):
+            acc_out = psum.tile([N, P], F32, name="acc_out%d" % s)
+            for w, src in (("w4", e_both[:, s]), ("w3", a_both[:, s])):
+                codes = tile("child_codes%d%s" % (s, w), [P, P], U32)
+                scales = tile("child_scales%d%s" % (s, w), [P, P], U8)
+                quantize(codes[:], scales[:], src.rearrange("p v t -> p (v t)"))
+                mx(acc_out[:], w_codes[w], w_scales[w], codes[:], scales[:], w == "w4")
+            result = tile("result%d" % s, [N, P], F32)
+            nc.scalar.activation(result[:], acc_out[:], GELU)
+            nc.sync.dma_start(out=out[:, s * P : (s + 1) * P], in_=result[:])

@@ -17,7 +17,7 @@ GELU = mybir.ActivationFunctionType.Gelu_apprx_tanh
 P = 128
 PACK = 4
 HALF = P // 2
-H_BYTES = 4 * S
+CUT = 96
 
 
 def tile_picked_yrecnn_gelu_p_kernel(
@@ -60,7 +60,6 @@ def tile_picked_yrecnn_gelu_p_kernel(
         offs_sb = load_list("offs_sb", offs)
         word_table = tile("word_table", [P, T], I32)
         nc.sync.dma_start(out=word_table[:], in_=x_words[0].rearrange("p n r -> p (n r)").bitcast(I32))
-        right_sb = load_list("right_sb", right)
         scale_table = tile("scale_table", [P, T], U8)
         nc.vector.memset(scale_table[:].bitcast(I32), 0)
         for q in range(4):
@@ -68,19 +67,20 @@ def tile_picked_yrecnn_gelu_p_kernel(
                 out=scale_table[32 * q : 32 * q + 4, :].bitcast(I32),
                 in_=x_scales[0, 4 * q : 4 * q + 4, :].bitcast(I32),
             )
+        right_sb = load_list("right_sb", right)
         w1_raw = [load_rows("w1_raw%d" % u, w1, slice(u * H // 2, (u + 1) * H // 2)) for u in range(2)]
-        w2_raw = [load_rows("w2_raw%d" % u, w2, slice(u * H // 2, (u + 1) * H // 2)) for u in range(2)]
-        w3_raw = reused.tile([P, PACK * N + 64], F32, name="w3_raw", align_bytes=64, offset=2 * H_BYTES - 128)
-        w4_raw = reused.tile([P, PACK * N], F32, name="w4_raw", align_bytes=64, offset=7 * H_BYTES // 2)
-        w34_raw = [raw[:, : PACK * N].rearrange("p (j c) -> p j c", j=PACK) for raw in (w3_raw, w4_raw)]
-        for raw, w in zip(w34_raw, (w3, w4)):
-            nc.sync.dma_start(out=raw, in_=w.rearrange("(p j) c -> p j c", j=PACK))
-        up1_sb = load_list("up1_sb", up1)
+        w2_cuts = [slice(0, HALF), slice(HALF, CUT), slice(CUT, P)]
+        w2_raw = [load_rows("w2_raw%d" % n, w2, slice(m.start * PACK, m.stop * PACK)) for n, m in enumerate(w2_cuts)]
+        w3_room = reused.tile([P, PACK * S], F32, name="w3_room", align_bytes=64, offset=0)
+        w3_raw = w3_room[:, : PACK * N].rearrange("p (j c) -> p j c", j=PACK)
+        nc.sync.dma_start(out=w3_raw, in_=w3.rearrange("(p j) c -> p j c", j=PACK))
+        w4_raw = load_rows("w4_raw", w4, slice(0, N))[:]
         up2_sb = load_list("up2_sb", up2)
+        up1_sb = load_list("up1_sb", up1)
 
         warm_in = tile("warm_in", [P, 8], F32)
         warm_out = tile("warm_out", [P, 8], F32)
-        nc.gpsimd.memset(warm_in[:], 0.0)
+        nc.vector.memset(warm_in[:], 0.0)
         nc.scalar.activation(warm_out[:], warm_in[:], GELU)
 
         def pick_words(name, lst):
@@ -93,14 +93,28 @@ def tile_picked_yrecnn_gelu_p_kernel(
             nc.vector.tensor_copy(sc[:], scale_table[:].indirect(lst[:]))
             return sc
 
-        picked = [[pick_words("left_words", offs_sb), pick_scales("left_scales", offs_sb)]]
-        right_words = pick_words("right_words", right_sb)
+        picked_words = [pick_words("left_words", offs_sb)]
+        picked_scales = [pick_scales("left_scales", offs_sb)]
+        picked_words.append(pick_words("right_words", right_sb))
 
-        grouped = [tile("grouped%d" % u, [P, PACK, P, PACK], BF16) for u in range(2)]
+        warm = psum.tile([P, S], F32, name="warm")
+        for n in range(2):
+            nc.tensor.matmul_mx(
+                out=warm[:],
+                lhsT=picked_words[0][:, :P].bitcast(FP8X4),
+                lhsT_scale=picked_scales[0][:, :P],
+                rhs=picked_words[0][:].bitcast(FP8X4),
+                rhs_scale=picked_scales[0][:],
+                start=True,
+                stop=True,
+            )
 
-        def group(engine_copy, raw, u, half, planes):
+        w1_grouped = tile("w1_grouped", [P, PACK, P, PACK], BF16)
+        w2_grouped = tile("w2_grouped", [P, PACK, P, PACK], BF16)
+
+        def group(engine_copy, dst, raw, planes):
             engine_copy(
-                grouped[u][:, planes, half * HALF : (half + 1) * HALF, :].rearrange("p t m j -> p m j t"),
+                dst.rearrange("p t m j -> p m j t"),
                 raw[:].rearrange("p j (m t) -> p m j t", t=PACK)[:, :, :, planes],
             )
 
@@ -116,85 +130,95 @@ def tile_picked_yrecnn_gelu_p_kernel(
                 w_scales[key] = scales[:, n * P : (n + 1) * P]
 
         spans = [[slice(0, S // 2), slice(S // 2, S)]] + [[slice(0, S)]] * (PACK - 1)
-        acc = [
-            [psum.tile([P, cols.stop - cols.start], F32, name="acc%d_%d" % (t, n)) for n, cols in enumerate(spans[t])]
-            for t in range(PACK)
-        ]
+        acc = {}
+
+        def open_banks(t):
+            acc[t] = [psum.tile([P, cols.stop - cols.start], F32, name="acc%d_%d" % (t, n), tag="acc%d_%d" % (min(t, PACK - t), n)) for n, cols in enumerate(spans[t])]
+
         h = []
 
         def first_level(t, u):
+            if u == 0:
+                open_banks(t)
             for n, cols in enumerate(spans[t]):
-                mx(acc[t][n][:], w_codes[t, u], w_scales[t, u], picked[u][0][:, cols], picked[u][1][:, cols], u == 0)
+                mx(acc[t][n][:], w_codes[t, u], w_scales[t, u], picked_words[u][:, cols], picked_scales[u][:, cols], u == 0)
 
         def activate(t):
-            h.append(reused.tile([P, S], F32, name="h%d" % t, align_bytes=64, offset=t * H_BYTES))
+            h.append(reused.tile([P, S], F32, name="h%d" % t, align_bytes=64, offset=t * 4 * S))
             for n, cols in enumerate(spans[t]):
                 nc.scalar.activation(h[t][:, cols], acc[t][n][:], GELU)
 
-        group(nc.scalar.copy, w1_raw[0], 0, 0, slice(0, 4))
-        group(nc.scalar.copy, w1_raw[1], 0, 1, slice(0, 4))
-        quantize_weights("w1_first", grouped[0][:, :2].rearrange("p t m j -> p (t m j)"), [(0, 0), (1, 0)])
+        group(nc.scalar.copy, w1_grouped[:, :, :HALF], w1_raw[0], slice(0, PACK))
+        for g in range(2):
+            group(nc.scalar.copy, w1_grouped[:, 2 * g : 2 * g + 2, HALF:], w1_raw[1], slice(2 * g, 2 * g + 2))
+
+        def left_pair(g, tag=""):
+            src = w1_grouped[:, 2 * g : 2 * g + 2].rearrange("p t m j -> p (t m j)")
+            quantize_weights("w1_%d" % g, src, [(2 * g, 0), (2 * g + 1, 0)], tag=tag)
+
+        left_pair(0)
         first_level(0, 0)
         first_level(1, 0)
-        picked.append([right_words, pick_scales("right_scales", right_sb, tag="w1_raw1")])
-        group(nc.scalar.copy, w2_raw[0], 1, 0, slice(0, 4))
-        group(nc.scalar.copy, w2_raw[1], 1, 1, slice(0, 2))
-        group(nc.scalar.copy, w2_raw[1], 1, 1, slice(2, 4))
-        quantize_weights("w2_first", grouped[1][:, 0].rearrange("p m j -> p (m j)"), [(0, 1)])
-        first_level(0, 1)
-        quantize_weights("w2_second", grouped[1][:, 1].rearrange("p m j -> p (m j)"), [(1, 1)])
-        first_level(1, 1)
-        quantize_weights("w1_rest", grouped[0][:, 2:].rearrange("p t m j -> p (t m j)"), [(2, 0), (3, 0)], tag="w2_raw1")
-        quantize_weights("w2_rest", grouped[1][:, 2:].rearrange("p t m j -> p (t m j)"), [(2, 1), (3, 1)])
-        for t in range(2, PACK):
-            first_level(t, 0)
-            first_level(t, 1)
-
-        w34_grouped = tile("w34_grouped", [P, 2, N, PACK], BF16)
-
-        def group_second(u):
-            nc.scalar.copy(
-                w34_grouped[:, u].rearrange("p (c i) j -> p c j i", i=4),
-                w34_raw[u].rearrange("p j (c i) -> p c j i", i=4),
-            )
-
-        activate(0)
-        group_second(0)
-        activate(1)
-        activate(2)
-        group_second(1)
-        activate(3)
-        quantize_weights("w34", w34_grouped[:].rearrange("p u c j -> p (u c j)"), ["w3", "w4"])
-
-        a_planes = tile("a_planes", [P, PACK, V], BF16, tag="grouped1")
-        e_planes = tile("e_planes", [P, 2, V], BF16)
-        e_both = reused.tile([P, 2, P, PACK], BF16, name="e_both", align_bytes=64, offset=4 * H_BYTES)
+        picked_scales.append(pick_scales("right_scales", right_sb, tag="w1_raw1"))
+        group(nc.scalar.copy, w2_grouped[:, :, w2_cuts[0]], w2_raw[0], slice(0, PACK))
+        for g in range(2):
+            pair = slice(2 * g, 2 * g + 2)
+            group(nc.scalar.copy, w2_grouped[:, pair, w2_cuts[1]], w2_raw[1], pair)
+            group(nc.vector.tensor_copy, w2_grouped[:, pair, w2_cuts[2]], w2_raw[2], pair)
         for t in range(2):
-            nc.vector.tensor_copy(a_planes[:, t], h[t][:].indirect(up1_sb[:]))
-            nc.vector.tensor_copy(e_planes[:, t], h[t][:].indirect(up2_sb[:]))
+            quantize_weights("w2_%d" % t, w2_grouped[:, t].rearrange("p m j -> p (m j)"), [(t, 1)])
+            first_level(t, 1)
+        left_pair(1, tag="w2_raw1")
+        quantize_weights("w2_rest", w2_grouped[:, 2:].rearrange("p t m j -> p (t m j)"), [(2, 1), (3, 1)])
+        first_level(2, 0)
+        first_level(2, 1)
+        staging = tile("staging", [P, PACK, V], BF16)
+        w34_grouped = staging[:].rearrange("p (u r) v -> p u (r v)", u=2)
+        for u, (engine_copy, raw) in enumerate(((nc.scalar.copy, w3_raw), (nc.vector.tensor_copy, w4_raw))):
+            engine_copy(
+                w34_grouped[:, u].rearrange("p (c i j) -> p c j i", i=4, j=PACK),
+                raw.rearrange("p j (c i) -> p c j i", i=4),
+            )
+        for u, w in enumerate(("w3", "w4")):
+            quantize_weights(w, w34_grouped[:, u], [w])
+        activate(0)
+        activate(1)
+        first_level(3, 0)
+        first_level(3, 1)
+        activate(2)
+        activate(3)
+
+        both = tile("both", [P, 2, 2, P, PACK], BF16)
+        for t in range(PACK - 1):
+            nc.vector.tensor_copy(staging[:, t], h[t][:].indirect(up2_sb[:]))
         nc.scalar.copy(
-            e_both[:, :, :, 0:2].rearrange("p s (c i) t -> p (s c) t i", i=4),
-            e_planes[:].rearrange("p t (c i) -> p c t i", i=4),
+            both[:, :, 1].rearrange("p s (c i) t -> p s c t i", i=4),
+            staging[:].rearrange("p t (s c i) -> p s c t i", s=2, i=4),
         )
-        for t in range(2, PACK):
+        a_planes = tile("a_planes", [P, PACK, V], BF16, tag="right_words")
+        for t in range(PACK - 1):
             nc.vector.tensor_copy(a_planes[:, t], h[t][:].indirect(up1_sb[:]))
-        a_both = tile("a_both", [P, 2, P, PACK], BF16)
         for s in range(2):
+            nc.vector.tensor_copy(a_planes[:, 3, s * P : (s + 1) * P], h[3][:].indirect(up1_sb[:, 8 * s : 8 * s + 8]))
             nc.scalar.copy(
-                a_both[:, s].rearrange("p (c i) t -> p c t i", i=4),
+                both[:, s, 0].rearrange("p (c i) t -> p c t i", i=4),
                 a_planes[:, :, s * P : (s + 1) * P].rearrange("p t (c i) -> p c t i", i=4),
             )
-        nc.vector.tensor_copy(e_both[:, :, :, 2].rearrange("p s v -> p (s v)"), h[2][:].indirect(up2_sb[:]))
         for s in range(2):
-            nc.vector.tensor_copy(e_both[:, s, :, 3], h[3][:].indirect(up2_sb[:, 8 * s : 8 * s + 8]))
+            nc.vector.tensor_copy(both[:, s, 1, :, 3], h[3][:].indirect(up2_sb[:, 8 * s : 8 * s + 8]))
 
-        for s in range(2):
+        for s, parts in enumerate(([(0, 2)], [(1, 2), (0, 1)])):
             acc_out = psum.tile([N, P], F32, name="acc_out%d" % s)
-            for w, src in (("w4", e_both[:, s]), ("w3", a_both[:, s])):
-                codes = tile("child_codes%d%s" % (s, w), [P, P], U32)
-                scales = tile("child_scales%d%s" % (s, w), [P, P], U8)
-                quantize(codes[:], scales[:], src.rearrange("p v t -> p (v t)"))
-                mx(acc_out[:], w_codes[w], w_scales[w], codes[:], scales[:], w == "w4")
+            passes = 0
+            for lo, hi in parts:
+                codes = tile("child_codes%d_%d" % (s, lo), [P, (hi - lo) * P], U32)
+                scales = tile("child_scales%d_%d" % (s, lo), [P, (hi - lo) * P], U8)
+                quantize(codes[:], scales[:], both[:, s, lo:hi].rearrange("p u v t -> p (u v t)"))
+                for u in range(lo, hi):
+                    cols = slice((u - lo) * P, (u - lo + 1) * P)
+                    w = ("w3", "w4")[u]
+                    mx(acc_out[:], w_codes[w], w_scales[w], codes[:, cols], scales[:, cols], passes == 0)
+                    passes = passes + 1
             result = tile("result%d" % s, [N, P], F32)
             nc.scalar.activation(result[:], acc_out[:], GELU)
             nc.sync.dma_start(out=out[:, s * P : (s + 1) * P], in_=result[:])

@@ -68,8 +68,8 @@ def tile_picked_yrecnn_gelu_p_kernel(
                 in_=x_scales[0, 4 * q : 4 * q + 4, :].bitcast(I32),
             )
         right_sb = load_list("right_sb", right)
-        w1_raw = [load_rows("w1_raw%d" % u, w1, slice(u * H // 2, (u + 1) * H // 2)) for u in range(2)]
         w2_cuts = [slice(0, HALF), slice(HALF, CUT), slice(CUT, P)]
+        w1_raw = [load_rows("w1_raw%d" % n, w1, slice(m.start * PACK, m.stop * PACK)) for n, m in enumerate(w2_cuts)]
         w2_raw = [load_rows("w2_raw%d" % n, w2, slice(m.start * PACK, m.stop * PACK)) for n, m in enumerate(w2_cuts)]
         w3_room = reused.tile([P, PACK * S], F32, name="w3_room", align_bytes=64, offset=0)
         w3_raw = w3_room[:, : PACK * N].rearrange("p (j c) -> p j c", j=PACK)
@@ -98,7 +98,7 @@ def tile_picked_yrecnn_gelu_p_kernel(
         picked_words.append(pick_words("right_words", right_sb))
 
         warm = psum.tile([P, S], F32, name="warm")
-        for n in range(2):
+        for n in range(1):
             nc.tensor.matmul_mx(
                 out=warm[:],
                 lhsT=picked_words[0][:, :P].bitcast(FP8X4),
@@ -150,19 +150,21 @@ def tile_picked_yrecnn_gelu_p_kernel(
 
         group(nc.scalar.copy, w1_grouped[:, :, :HALF], w1_raw[0], slice(0, PACK))
         for g in range(2):
-            group(nc.scalar.copy, w1_grouped[:, 2 * g : 2 * g + 2, HALF:], w1_raw[1], slice(2 * g, 2 * g + 2))
+            pair = slice(2 * g, 2 * g + 2)
+            for n in (1, 2):
+                group(nc.scalar.copy, w1_grouped[:, pair, w2_cuts[n]], w1_raw[n], pair)
 
         def left_pair(g, tag=""):
             src = w1_grouped[:, 2 * g : 2 * g + 2].rearrange("p t m j -> p (t m j)")
             quantize_weights("w1_%d" % g, src, [(2 * g, 0), (2 * g + 1, 0)], tag=tag)
 
-        left_pair(0)
-        first_level(0, 0)
-        first_level(1, 0)
+        for t in range(2):
+            quantize_weights("w1_%d_alone" % t, w1_grouped[:, t].rearrange("p m j -> p (m j)"), [(t, 0)])
+            first_level(t, 0)
         picked_scales.append(pick_scales("right_scales", right_sb, tag="w1_raw1"))
-        group(nc.scalar.copy, w2_grouped[:, :, w2_cuts[0]], w2_raw[0], slice(0, PACK))
         for g in range(2):
             pair = slice(2 * g, 2 * g + 2)
+            group(nc.scalar.copy, w2_grouped[:, pair, w2_cuts[0]], w2_raw[0], pair)
             group(nc.scalar.copy, w2_grouped[:, pair, w2_cuts[1]], w2_raw[1], pair)
             group(nc.vector.tensor_copy, w2_grouped[:, pair, w2_cuts[2]], w2_raw[2], pair)
         for t in range(2):
@@ -173,14 +175,15 @@ def tile_picked_yrecnn_gelu_p_kernel(
         first_level(2, 0)
         first_level(2, 1)
         staging = tile("staging", [P, PACK, V], BF16)
-        w34_grouped = staging[:].rearrange("p (u r) v -> p u (r v)", u=2)
-        for u, (engine_copy, raw) in enumerate(((nc.scalar.copy, w3_raw), (nc.vector.tensor_copy, w4_raw))):
+        w3_grouped = tile("w3_grouped", [P, N * PACK], BF16)[:]
+        w4_grouped = staging[:, 2:].rearrange("p r v -> p (r v)")
+        for engine_copy, dst, raw in ((nc.scalar.copy, w3_grouped, w3_raw), (nc.vector.tensor_copy, w4_grouped, w4_raw)):
             engine_copy(
-                w34_grouped[:, u].rearrange("p (c i j) -> p c j i", i=4, j=PACK),
+                dst.rearrange("p (c i j) -> p c j i", i=4, j=PACK),
                 raw.rearrange("p j (c i) -> p c j i", i=4),
             )
-        for u, w in enumerate(("w3", "w4")):
-            quantize_weights(w, w34_grouped[:, u], [w])
+        quantize_weights("w3", w3_grouped, ["w3"])
+        quantize_weights("w4", w4_grouped, ["w4"])
         activate(0)
         activate(1)
         first_level(3, 0)

@@ -97,18 +97,6 @@ def tile_picked_yrecnn_gelu_p_kernel(
         picked_scales = [pick_scales("left_scales", offs_sb)]
         picked_words.append(pick_words("right_words", right_sb))
 
-        warm = psum.tile([P, S], F32, name="warm")
-        for n in range(1):
-            nc.tensor.matmul_mx(
-                out=warm[:],
-                lhsT=picked_words[0][:, :P].bitcast(FP8X4),
-                lhsT_scale=picked_scales[0][:, :P],
-                rhs=picked_words[0][:].bitcast(FP8X4),
-                rhs_scale=picked_scales[0][:],
-                start=True,
-                stop=True,
-            )
-
         w1_grouped = tile("w1_grouped", [P, PACK, P, PACK], BF16)
         w2_grouped = tile("w2_grouped", [P, PACK, P, PACK], BF16)
 
@@ -129,7 +117,7 @@ def tile_picked_yrecnn_gelu_p_kernel(
                 w_codes[key] = codes[:, n * P : (n + 1) * P]
                 w_scales[key] = scales[:, n * P : (n + 1) * P]
 
-        spans = [[slice(0, S // 2), slice(S // 2, S)]] + [[slice(0, S)]] * (PACK - 1)
+        spans = [[slice(0, S // 2), slice(S // 2, S)]] * PACK
         acc = {}
 
         def open_banks(t):
@@ -201,27 +189,37 @@ def tile_picked_yrecnn_gelu_p_kernel(
         a_planes = tile("a_planes", [P, PACK, V], BF16, tag="right_words")
         for t in range(PACK - 1):
             nc.vector.tensor_copy(a_planes[:, t], h[t][:].indirect(up1_sb[:]))
-        for s in range(2):
+        acc_out = [psum.tile([N, P], F32, name="acc_out%d" % s) for s in range(2)]
+
+        def last_a_plane(s):
             nc.vector.tensor_copy(a_planes[:, 3, s * P : (s + 1) * P], h[3][:].indirect(up1_sb[:, 8 * s : 8 * s + 8]))
             nc.scalar.copy(
                 both[:, s, 0].rearrange("p (c i) t -> p c t i", i=4),
                 a_planes[:, :, s * P : (s + 1) * P].rearrange("p t (c i) -> p c t i", i=4),
             )
-        for s in range(2):
+
+        def last_e_plane(s):
             nc.vector.tensor_copy(both[:, s, 1, :, 3], h[3][:].indirect(up2_sb[:, 8 * s : 8 * s + 8]))
 
-        for s, parts in enumerate(([(0, 2)], [(1, 2), (0, 1)])):
-            acc_out = psum.tile([N, P], F32, name="acc_out%d" % s)
-            passes = 0
-            for lo, hi in parts:
-                codes = tile("child_codes%d_%d" % (s, lo), [P, (hi - lo) * P], U32)
-                scales = tile("child_scales%d_%d" % (s, lo), [P, (hi - lo) * P], U8)
-                quantize(codes[:], scales[:], both[:, s, lo:hi].rearrange("p u v t -> p (u v t)"))
-                for u in range(lo, hi):
-                    cols = slice((u - lo) * P, (u - lo + 1) * P)
-                    w = ("w3", "w4")[u]
-                    mx(acc_out[:], w_codes[w], w_scales[w], codes[:, cols], scales[:, cols], passes == 0)
-                    passes = passes + 1
+        def second_level(s, u):
+            codes = tile("child_codes%d_%d" % (s, u), [P, P], U32)
+            scales = tile("child_scales%d_%d" % (s, u), [P, P], U8)
+            quantize(codes[:], scales[:], both[:, s, u].rearrange("p v t -> p (v t)"))
+            w = ("w3", "w4")[u]
+            mx(acc_out[s][:], w_codes[w], w_scales[w], codes[:], scales[:], u == 1)
+
+        def finish(s):
             result = tile("result%d" % s, [N, P], F32)
-            nc.scalar.activation(result[:], acc_out[:], GELU)
-            nc.sync.dma_start(out=out[:, s * P : (s + 1) * P], in_=result[:])
+            nc.scalar.activation(result[:], acc_out[s][:], GELU)
+            (nc.sync, nc.scalar)[s].dma_start(out=out[:, s * P : (s + 1) * P], in_=result[:])
+
+        last_a_plane(0)
+        last_a_plane(1)
+        last_e_plane(0)
+        last_e_plane(1)
+        second_level(0, 1)
+        second_level(0, 0)
+        second_level(1, 1)
+        finish(0)
+        second_level(1, 0)
+        finish(1)

@@ -97,6 +97,18 @@ def tile_picked_yrecnn_gelu_p_kernel(
         picked_scales = [pick_scales("left_scales", offs_sb)]
         picked_words.append(pick_words("right_words", right_sb))
 
+        warm = psum.tile([P, S], F32, name="warm", tag="acc2_0")
+        for n in range(2):
+            nc.tensor.matmul_mx(
+                out=warm[:],
+                lhsT=picked_words[0][:, :P].bitcast(FP8X4),
+                lhsT_scale=picked_scales[0][:, :P],
+                rhs=picked_words[0][:].bitcast(FP8X4),
+                rhs_scale=picked_scales[0][:],
+                start=True,
+                stop=True,
+            )
+
         w1_grouped = tile("w1_grouped", [P, PACK, P, PACK], BF16)
         w2_grouped = tile("w2_grouped", [P, PACK, P, PACK], BF16)
 

@@ -68,9 +68,9 @@ def tile_picked_yrecnn_gelu_p_kernel(
                 in_=x_scales[0, 4 * q : 4 * q + 4, :].bitcast(I32),
             )
         right_sb = load_list("right_sb", right)
-        w2_cuts = [slice(0, HALF), slice(HALF, CUT), slice(CUT, P)]
-        w1_raw = [load_rows("w1_raw%d" % n, w1, slice(m.start * PACK, m.stop * PACK)) for n, m in enumerate(w2_cuts)]
-        w2_raw = [load_rows("w2_raw%d" % n, w2, slice(m.start * PACK, m.stop * PACK)) for n, m in enumerate(w2_cuts)]
+        halves = [slice(0, HALF), slice(HALF, P)]
+        w1_raw = [load_rows("w1_raw%d" % n, w1, slice(m.start * PACK, m.stop * PACK)) for n, m in enumerate(halves)]
+        w2_raw = [load_rows("w2_raw%d" % n, w2, slice(m.start * PACK, m.stop * PACK)) for n, m in enumerate(halves)]
         w3_room = reused.tile([P, PACK * S], F32, name="w3_room", align_bytes=64, offset=0)
         w3_raw = w3_room[:, : PACK * N].rearrange("p (j c) -> p j c", j=PACK)
         nc.sync.dma_start(out=w3_raw, in_=w3.rearrange("(p j) c -> p j c", j=PACK))
@@ -98,24 +98,27 @@ def tile_picked_yrecnn_gelu_p_kernel(
         picked_words.append(pick_words("right_words", right_sb))
 
         warm = psum.tile([P, S], F32, name="warm", tag="acc2_0")
-        for n in range(2):
+
+        def warm_up(u):
             nc.tensor.matmul_mx(
                 out=warm[:],
-                lhsT=picked_words[0][:, :P].bitcast(FP8X4),
-                lhsT_scale=picked_scales[0][:, :P],
-                rhs=picked_words[0][:].bitcast(FP8X4),
-                rhs_scale=picked_scales[0][:],
+                lhsT=picked_words[u][:, :P].bitcast(FP8X4),
+                lhsT_scale=picked_scales[u][:, :P],
+                rhs=picked_words[u][:].bitcast(FP8X4),
+                rhs_scale=picked_scales[u][:],
                 start=True,
                 stop=True,
             )
 
+        warm_up(0)
+
         w1_grouped = tile("w1_grouped", [P, PACK, P, PACK], BF16)
         w2_grouped = tile("w2_grouped", [P, PACK, P, PACK], BF16)
 
-        def group(engine_copy, dst, raw, planes):
+        def group(engine_copy, dst, raw, planes, cols=slice(0, HALF)):
             engine_copy(
                 dst.rearrange("p t m j -> p m j t"),
-                raw[:].rearrange("p j (m t) -> p m j t", t=PACK)[:, :, :, planes],
+                raw[:].rearrange("p j (m t) -> p m j t", t=PACK)[:, cols, :, planes],
             )
 
         w_codes = {}
@@ -151,8 +154,7 @@ def tile_picked_yrecnn_gelu_p_kernel(
         group(nc.scalar.copy, w1_grouped[:, :, :HALF], w1_raw[0], slice(0, PACK))
         for g in range(2):
             pair = slice(2 * g, 2 * g + 2)
-            for n in (1, 2):
-                group(nc.scalar.copy, w1_grouped[:, pair, w2_cuts[n]], w1_raw[n], pair)
+            group(nc.scalar.copy, w1_grouped[:, pair, HALF:], w1_raw[1], pair)
 
         def left_pair(g, tag=""):
             src = w1_grouped[:, 2 * g : 2 * g + 2].rearrange("p t m j -> p (t m j)")
@@ -162,11 +164,12 @@ def tile_picked_yrecnn_gelu_p_kernel(
             quantize_weights("w1_%d_alone" % t, w1_grouped[:, t].rearrange("p m j -> p (m j)"), [(t, 0)])
             first_level(t, 0)
         picked_scales.append(pick_scales("right_scales", right_sb, tag="w1_raw1"))
+        warm_up(1)
         for g in range(2):
             pair = slice(2 * g, 2 * g + 2)
-            group(nc.scalar.copy, w2_grouped[:, pair, w2_cuts[0]], w2_raw[0], pair)
-            group(nc.scalar.copy, w2_grouped[:, pair, w2_cuts[1]], w2_raw[1], pair)
-            group(nc.vector.tensor_copy, w2_grouped[:, pair, w2_cuts[2]], w2_raw[2], pair)
+            group(nc.scalar.copy, w2_grouped[:, pair, :HALF], w2_raw[0], pair)
+            group(nc.scalar.copy, w2_grouped[:, pair, HALF:CUT], w2_raw[1], pair, slice(0, CUT - HALF))
+            group(nc.vector.tensor_copy, w2_grouped[:, pair, CUT:], w2_raw[1], pair, slice(CUT - HALF, HALF))
         for t in range(2):
             quantize_weights("w2_%d" % t, w2_grouped[:, t].rearrange("p m j -> p (m j)"), [(t, 1)])
             first_level(t, 1)
@@ -174,16 +177,18 @@ def tile_picked_yrecnn_gelu_p_kernel(
         quantize_weights("w2_rest", w2_grouped[:, 2:].rearrange("p t m j -> p (t m j)"), [(2, 1), (3, 1)])
         first_level(2, 0)
         first_level(2, 1)
-        staging = tile("staging", [P, PACK, V], BF16)
-        w3_grouped = tile("w3_grouped", [P, N * PACK], BF16)[:]
-        w4_grouped = staging[:, 2:].rearrange("p r v -> p (r v)")
+        staging = tile("staging", [P, PACK + 1, V], BF16)
+        w3_grouped = staging[:, 3:].rearrange("p r v -> p (r v)")
+        woven = tile("woven", [P, 5, P, PACK], BF16)
+        w4_grouped = woven[:, 0].rearrange("p v t -> p (v t)")
+        e_woven = woven[:, 1:3]
+        a_woven = woven[:, 3:5]
         for engine_copy, dst, raw in ((nc.scalar.copy, w3_grouped, w3_raw), (nc.vector.tensor_copy, w4_grouped, w4_raw)):
             engine_copy(
                 dst.rearrange("p (c i j) -> p c j i", i=4, j=PACK),
                 raw.rearrange("p j (c i) -> p c j i", i=4),
             )
         quantize_weights("w3", w3_grouped, ["w3"])
-        quantize_weights("w4", w4_grouped, ["w4"])
         activate(0)
         activate(1)
         first_level(3, 0)
@@ -191,12 +196,11 @@ def tile_picked_yrecnn_gelu_p_kernel(
         activate(2)
         activate(3)
 
-        both = tile("both", [P, 2, 2, P, PACK], BF16)
         for t in range(PACK - 1):
             nc.vector.tensor_copy(staging[:, t], h[t][:].indirect(up2_sb[:]))
         nc.scalar.copy(
-            both[:, :, 1].rearrange("p s (c i) t -> p s c t i", i=4),
-            staging[:].rearrange("p t (s c i) -> p s c t i", s=2, i=4),
+            e_woven.rearrange("p s (c i) t -> p s c t i", i=4),
+            staging[:, :PACK].rearrange("p t (s c i) -> p s c t i", s=2, i=4),
         )
         a_planes = tile("a_planes", [P, PACK, V], BF16, tag="right_words")
         for t in range(PACK - 1):
@@ -206,19 +210,19 @@ def tile_picked_yrecnn_gelu_p_kernel(
         def last_a_plane(s):
             nc.vector.tensor_copy(a_planes[:, 3, s * P : (s + 1) * P], h[3][:].indirect(up1_sb[:, 8 * s : 8 * s + 8]))
             nc.scalar.copy(
-                both[:, s, 0].rearrange("p (c i) t -> p c t i", i=4),
+                a_woven[:, s].rearrange("p (c i) t -> p c t i", i=4),
                 a_planes[:, :, s * P : (s + 1) * P].rearrange("p t (c i) -> p c t i", i=4),
             )
 
         def last_e_plane(s):
-            nc.vector.tensor_copy(both[:, s, 1, :, 3], h[3][:].indirect(up2_sb[:, 8 * s : 8 * s + 8]))
+            nc.vector.tensor_copy(e_woven[:, s, :, 3], h[3][:].indirect(up2_sb[:, 8 * s : 8 * s + 8]))
 
         def second_level(s, u):
-            codes = tile("child_codes%d_%d" % (s, u), [P, P], U32)
-            scales = tile("child_scales%d_%d" % (s, u), [P, P], U8)
-            quantize(codes[:], scales[:], both[:, s, u].rearrange("p v t -> p (v t)"))
             w = ("w3", "w4")[u]
-            mx(acc_out[s][:], w_codes[w], w_scales[w], codes[:], scales[:], u == 1)
+            mx(acc_out[s][:], w_codes[w], w_scales[w], w_codes["child", s, u], w_scales["child", s, u], u == 1)
+
+        def quantize_rows(name, rows, keys):
+            quantize_weights(name, woven[:, rows].rearrange("p r v t -> p (r v t)"), keys)
 
         def finish(s):
             result = tile("result%d" % s, [N, P], F32)
@@ -229,9 +233,13 @@ def tile_picked_yrecnn_gelu_p_kernel(
         last_a_plane(1)
         last_e_plane(0)
         last_e_plane(1)
+        quantize_rows("w4_e0", slice(0, 2), ["w4", ("child", 0, 1)])
         second_level(0, 1)
+        quantize_rows("a0", slice(3, 4), [("child", 0, 0)])
         second_level(0, 0)
+        quantize_rows("e1", slice(2, 3), [("child", 1, 1)])
         second_level(1, 1)
         finish(0)
+        quantize_rows("a1", slice(4, 5), [("child", 1, 0)])
         second_level(1, 0)
         finish(1)

@@ -13,11 +13,11 @@ U16 = mybir.dt.uint16
 U8 = mybir.dt.uint8
 FP8X4 = mybir.dt.float8_e4m3fn_x4
 GELU = mybir.ActivationFunctionType.Gelu_apprx_tanh
+COPY = mybir.ActivationFunctionType.Copy
 
 P = 128
 PACK = 4
 HALF = P // 2
-CUT = 96
 
 
 def tile_picked_yrecnn_gelu_p_kernel(
@@ -27,7 +27,6 @@ def tile_picked_yrecnn_gelu_p_kernel(
     with ExitStack() as ctx:
         lists = ctx.enter_context(tc.tile_pool(name="lists", bufs=1))
         sb = ctx.enter_context(tc.tile_pool(name="sb", bufs=1))
-        reused = ctx.enter_context(tc.tile_pool(name="reused", bufs=1))
         psum = ctx.enter_context(tc.psum_pool(name="psum", bufs=1))
 
         def tile(name, shape, dtype, tag=""):
@@ -43,18 +42,24 @@ def tile_picked_yrecnn_gelu_p_kernel(
             nc.sync.dma_start(out=dst[:], in_=w.rearrange("(p j) c -> p j c", j=PACK)[:, :, cols])
             return dst
 
-        def quantize(codes, scales, grouped):
-            nc.vector.quantize_mx(out=codes.bitcast(FP8X4), scales=scales, in_=grouped)
+        operands = {}
 
-        def mx(acc, w_codes, w_scales, x_codes, x_sc, first):
+        def quantize(name, src, keys, tag=""):
+            codes = tile(name + "_codes", [P, len(keys) * P], U32, tag=tag)
+            scales = tile(name + "_scales", [P, len(keys) * P], U8)
+            nc.vector.quantize_mx(out=codes[:].bitcast(FP8X4), scales=scales[:], in_=src)
+            for n, key in enumerate(keys):
+                operands[key] = (codes[:, n * P : (n + 1) * P], scales[:, n * P : (n + 1) * P])
+
+        def mx(acc, stationary, moving, start, stop):
             nc.tensor.matmul_mx(
                 out=acc,
-                lhsT=w_codes.bitcast(FP8X4),
-                lhsT_scale=w_scales,
-                rhs=x_codes.bitcast(FP8X4),
-                rhs_scale=x_sc,
-                start=first,
-                stop=not first,
+                lhsT=stationary[0].bitcast(FP8X4),
+                lhsT_scale=stationary[1],
+                rhs=moving[0].bitcast(FP8X4),
+                rhs_scale=moving[1],
+                start=start,
+                stop=stop,
             )
 
         offs_sb = load_list("offs_sb", offs)
@@ -68,13 +73,18 @@ def tile_picked_yrecnn_gelu_p_kernel(
                 in_=x_scales[0, 4 * q : 4 * q + 4, :].bitcast(I32),
             )
         right_sb = load_list("right_sb", right)
-        halves = [slice(0, HALF), slice(HALF, P)]
-        w1_raw = [load_rows("w1_raw%d" % n, w1, slice(m.start * PACK, m.stop * PACK)) for n, m in enumerate(halves)]
-        w2_raw = [load_rows("w2_raw%d" % n, w2, slice(m.start * PACK, m.stop * PACK)) for n, m in enumerate(halves)]
-        w3_room = reused.tile([P, PACK * S], F32, name="w3_room", align_bytes=64, offset=0)
-        w3_raw = w3_room[:, : PACK * N].rearrange("p (j c) -> p j c", j=PACK)
-        nc.sync.dma_start(out=w3_raw, in_=w3.rearrange("(p j) c -> p j c", j=PACK))
-        w4_raw = load_rows("w4_raw", w4, slice(0, N))[:]
+        halves = [slice(0, H // 2), slice(H // 2, H)]
+        w1_raw = [load_rows("w1_raw%d" % n, w1, cols) for n, cols in enumerate(halves)]
+        w2_raw = [load_rows("w2_raw%d" % n, w2, cols) for n, cols in enumerate(halves)]
+
+        def load_dealt(name, w):
+            dst = tile(name, [P, PACK, N], F32)
+            for i in range(2):
+                nc.sync.dma_start(out=dst[i:P:2], in_=w.rearrange("(g t i) c -> i g t c", t=PACK, i=2)[i])
+            return dst[:]
+
+        w4_raw = load_dealt("w4_raw", w4)
+        w3_raw = load_dealt("w3_raw", w3)
         up2_sb = load_list("up2_sb", up2)
         up1_sb = load_list("up1_sb", up1)
 
@@ -95,151 +105,117 @@ def tile_picked_yrecnn_gelu_p_kernel(
 
         picked_words = [pick_words("left_words", offs_sb)]
         picked_scales = [pick_scales("left_scales", offs_sb)]
-        picked_words.append(pick_words("right_words", right_sb))
-
-        warm = psum.tile([P, S], F32, name="warm", tag="acc2_0")
-
-        def warm_up(u):
-            nc.tensor.matmul_mx(
-                out=warm[:],
-                lhsT=picked_words[u][:, :P].bitcast(FP8X4),
-                lhsT_scale=picked_scales[u][:, :P],
-                rhs=picked_words[u][:].bitcast(FP8X4),
-                rhs_scale=picked_scales[u][:],
-                start=True,
-                stop=True,
+        right_words = tile("right_words", [P, S], U32)
+        picked_words.append(right_words)
+        for n in range(2):
+            nc.vector.tensor_copy(
+                right_words[:, n * V : (n + 1) * V],
+                word_table[:].bitcast(U32).indirect(right_sb[:, 16 * n : 16 * (n + 1)]),
             )
 
-        warm_up(0)
+        def picked(u, cols):
+            return (picked_words[u][:, cols], picked_scales[u][:, cols])
 
-        w1_grouped = tile("w1_grouped", [P, PACK, P, PACK], BF16)
-        w2_grouped = tile("w2_grouped", [P, PACK, P, PACK], BF16)
+        warm = psum.tile([P, S], F32, name="warm")
+        for start, width in ((0, 256), (256, 128), (384, 64)):
+            moving = (right_words[:, :width], picked_scales[0][:, :width])
+            mx(warm[:, start : start + width], picked(0, slice(0, P)), moving, True, True)
 
-        def group(engine_copy, dst, raw, planes, cols=slice(0, HALF)):
-            engine_copy(
-                dst.rearrange("p t m j -> p m j t"),
-                raw[:].rearrange("p j (m t) -> p m j t", t=PACK)[:, cols, :, planes],
-            )
+        early = [tile("early%d" % u, [P, 2, P, PACK], BF16) for u in range(2)]
+        late = tile("late", [P, 2, 2, P, PACK], BF16)
 
-        w_codes = {}
-        w_scales = {}
 
-        def quantize_weights(name, src, keys, tag=""):
-            codes = tile(name + "_codes", [P, len(keys) * P], U32, tag=tag)
-            scales = tile(name + "_scales", [P, len(keys) * P], U8)
-            quantize(codes[:], scales[:], src)
-            for n, key in enumerate(keys):
-                w_codes[key] = codes[:, n * P : (n + 1) * P]
-                w_scales[key] = scales[:, n * P : (n + 1) * P]
-
-        spans = [[slice(0, S // 2), slice(S // 2, S)]] * PACK
+        spans = [[slice(0, S // 2), slice(S // 2, S)]] + [[slice(0, S)]] * (PACK - 1)
         acc = {}
-
-        def open_banks(t):
-            acc[t] = [psum.tile([P, cols.stop - cols.start], F32, name="acc%d_%d" % (t, n), tag="acc%d_%d" % (min(t, PACK - t), n)) for n, cols in enumerate(spans[t])]
-
         h = []
 
         def first_level(t, u):
             if u == 0:
-                open_banks(t)
+                acc[t] = [
+                    psum.tile([P, cols.stop - cols.start], F32, name="acc%d_%d" % (t, n))
+                    for n, cols in enumerate(spans[t])
+                ]
             for n, cols in enumerate(spans[t]):
-                mx(acc[t][n][:], w_codes[t, u], w_scales[t, u], picked_words[u][:, cols], picked_scales[u][:, cols], u == 0)
+                mx(acc[t][n][:], operands[t, u], picked(u, cols), u == 0, u == 1)
 
         def activate(t):
-            h.append(reused.tile([P, S], F32, name="h%d" % t, align_bytes=64, offset=t * 4 * S))
+            h.append(tile("h%d" % t, [P, S], F32))
             for n, cols in enumerate(spans[t]):
                 nc.scalar.activation(h[t][:, cols], acc[t][n][:], GELU)
 
-        group(nc.scalar.copy, w1_grouped[:, :, :HALF], w1_raw[0], slice(0, PACK))
-        for g in range(2):
-            pair = slice(2 * g, 2 * g + 2)
-            group(nc.scalar.copy, w1_grouped[:, pair, HALF:], w1_raw[1], pair)
+        def cast(u, half, planes):
+            dst = early[u][:, planes] if planes.start < 2 else late[:, :, u]
+            raw = (w1_raw, w2_raw)[u][half]
+            if u == 0 and planes.start == 2:
+                nc.gpsimd.tensor_scalar(
+                    dst[:, :, half * HALF : (half + 1) * HALF].rearrange("p t (g i) j -> p g t i j", i=2),
+                    raw[:].rearrange("p j (g t i) -> p g t i j", t=PACK, i=2)[:, :, planes],
+                    1.0,
+                    0.0,
+                    mybir.AluOpType.mult,
+                    mybir.AluOpType.add,
+                )
+                return
+            nc.scalar.copy(
+                dst[:, :, half * HALF : (half + 1) * HALF].rearrange("p t (g i) j -> p g j t i", i=2),
+                raw[:].rearrange("p j (g t i) -> p g j t i", t=PACK, i=2)[:, :, :, planes],
+            )
 
-        def left_pair(g, tag=""):
-            src = w1_grouped[:, 2 * g : 2 * g + 2].rearrange("p t m j -> p (t m j)")
-            quantize_weights("w1_%d" % g, src, [(2 * g, 0), (2 * g + 1, 0)], tag=tag)
+        def cast_matrix(u):
+            for planes in (slice(0, 2), slice(2, 4)):
+                cast(u, 0, planes)
+            for planes in (slice(0, 1), slice(1, 2), slice(2, 4)):
+                cast(u, 1, planes)
 
+        cast_matrix(0)
         for t in range(2):
-            quantize_weights("w1_%d_alone" % t, w1_grouped[:, t].rearrange("p m j -> p (m j)"), [(t, 0)])
+            quantize("w1_%d" % t, early[0][:, t].rearrange("p m j -> p (m j)"), [(t, 0)])
             first_level(t, 0)
         picked_scales.append(pick_scales("right_scales", right_sb, tag="w1_raw1"))
-        warm_up(1)
-        for g in range(2):
-            pair = slice(2 * g, 2 * g + 2)
-            group(nc.scalar.copy, w2_grouped[:, pair, :HALF], w2_raw[0], pair)
-            group(nc.scalar.copy, w2_grouped[:, pair, HALF:CUT], w2_raw[1], pair, slice(0, CUT - HALF))
-            group(nc.vector.tensor_copy, w2_grouped[:, pair, CUT:], w2_raw[1], pair, slice(CUT - HALF, HALF))
+        cast_matrix(1)
         for t in range(2):
-            quantize_weights("w2_%d" % t, w2_grouped[:, t].rearrange("p m j -> p (m j)"), [(t, 1)])
+            quantize("w2_%d" % t, early[1][:, t].rearrange("p m j -> p (m j)"), [(t, 1)])
             first_level(t, 1)
-        left_pair(1, tag="w2_raw1")
-        quantize_weights("w2_rest", w2_grouped[:, 2:].rearrange("p t m j -> p (t m j)"), [(2, 1), (3, 1)])
-        first_level(2, 0)
-        first_level(2, 1)
-        staging = tile("staging", [P, PACK + 1, V], BF16)
-        w3_grouped = staging[:, 3:].rearrange("p r v -> p (r v)")
-        woven = tile("woven", [P, 5, P, PACK], BF16)
-        w4_grouped = woven[:, 0].rearrange("p v t -> p (v t)")
-        e_woven = woven[:, 1:3]
-        a_woven = woven[:, 3:5]
-        for engine_copy, dst, raw in ((nc.scalar.copy, w3_grouped, w3_raw), (nc.vector.tensor_copy, w4_grouped, w4_raw)):
-            engine_copy(
-                dst.rearrange("p (c i j) -> p c j i", i=4, j=PACK),
-                raw.rearrange("p j (c i) -> p c j i", i=4),
-            )
-        quantize_weights("w3", w3_grouped, ["w3"])
-        activate(0)
-        activate(1)
-        first_level(3, 0)
-        first_level(3, 1)
-        activate(2)
-        activate(3)
+        for t in range(2, PACK):
+            quantize("late_%d" % t, late[:, t - 2].rearrange("p u m j -> p (u m j)"), [(t, 0), (t, 1)])
+            first_level(t, 0)
+            first_level(t, 1)
+        for t in range(PACK):
+            activate(t)
 
-        for t in range(PACK - 1):
-            nc.vector.tensor_copy(staging[:, t], h[t][:].indirect(up2_sb[:]))
-        nc.scalar.copy(
-            e_woven.rearrange("p s (c i) t -> p s c t i", i=4),
-            staging[:, :PACK].rearrange("p t (s c i) -> p s c t i", s=2, i=4),
-        )
+        def weave(engine_copy, dst, planes):
+            engine_copy(
+                dst.rearrange("p (c i) t -> p c t i", i=4),
+                planes.rearrange("p t (c i) -> p c t i", i=4),
+            )
+
+        w34_grouped = tile("w34_grouped", [P, 2, N, PACK], BF16, tag="late")
+        for n, raw in enumerate((w4_raw, w3_raw)):
+            nc.gpsimd.tensor_scalar(
+                w34_grouped[:, n], raw.rearrange("p j c -> p c j"), 1.0, 0.0, mybir.AluOpType.mult, mybir.AluOpType.add
+            )
+
+        e_planes = tile("e_planes", [P, PACK, V], BF16)
         a_planes = tile("a_planes", [P, PACK, V], BF16, tag="right_words")
+        for t in range(PACK):
+            nc.vector.tensor_copy(e_planes[:, t], h[t][:].indirect(up2_sb[:]))
         for t in range(PACK - 1):
-            nc.vector.tensor_copy(a_planes[:, t], h[t][:].indirect(up1_sb[:]))
+            nc.scalar.activation(a_planes[:, t], h[t][:].indirect(up1_sb[:]), COPY)
+        nc.vector.tensor_copy(a_planes[:, 3], h[3][:].indirect(up1_sb[:]))
+        e_woven = tile("e_woven", [P, V, PACK], BF16)
+        weave(nc.vector.tensor_copy, e_woven[:], e_planes[:])
+        quantize("w34", w34_grouped[:].rearrange("p u c j -> p (u c j)"), ["w4", "w3"], tag="h1")
+        a_woven = [tile("a_woven%d" % s, [P, P, PACK], BF16) for s in range(2)]
+        weave(nc.scalar.copy, a_woven[0][:], a_planes[:, :, :P])
+        weave(nc.vector.tensor_copy, a_woven[1][:], a_planes[:, :, P:])
         acc_out = [psum.tile([N, P], F32, name="acc_out%d" % s) for s in range(2)]
 
-        def last_a_plane(s):
-            nc.vector.tensor_copy(a_planes[:, 3, s * P : (s + 1) * P], h[3][:].indirect(up1_sb[:, 8 * s : 8 * s + 8]))
-            nc.scalar.copy(
-                a_woven[:, s].rearrange("p (c i) t -> p c t i", i=4),
-                a_planes[:, :, s * P : (s + 1) * P].rearrange("p t (c i) -> p c t i", i=4),
-            )
-
-        def last_e_plane(s):
-            nc.vector.tensor_copy(e_woven[:, s, :, 3], h[3][:].indirect(up2_sb[:, 8 * s : 8 * s + 8]))
-
-        def second_level(s, u):
-            w = ("w3", "w4")[u]
-            mx(acc_out[s][:], w_codes[w], w_scales[w], w_codes["child", s, u], w_scales["child", s, u], u == 1)
-
-        def quantize_rows(name, rows, keys):
-            quantize_weights(name, woven[:, rows].rearrange("p r v t -> p (r v t)"), keys)
-
-        def finish(s):
+        quantize("e", e_woven[:].rearrange("p v t -> p (v t)"), [("e", 0), ("e", 1)])
+        for s in range(2):
+            mx(acc_out[s][:], operands["w4"], operands["e", s], True, False)
+        for s in (1, 0):
+            quantize("a%d" % s, a_woven[s][:].rearrange("p v t -> p (v t)"), [("a", s)])
+            mx(acc_out[s][:], operands["w3"], operands["a", s], False, True)
             result = tile("result%d" % s, [N, P], F32)
             nc.scalar.activation(result[:], acc_out[s][:], GELU)
-            (nc.sync, nc.scalar)[s].dma_start(out=out[:, s * P : (s + 1) * P], in_=result[:])
-
-        last_a_plane(0)
-        last_a_plane(1)
-        last_e_plane(0)
-        last_e_plane(1)
-        quantize_rows("w4_e0", slice(0, 2), ["w4", ("child", 0, 1)])
-        second_level(0, 1)
-        quantize_rows("a0", slice(3, 4), [("child", 0, 0)])
-        second_level(0, 0)
-        quantize_rows("e1", slice(2, 3), [("child", 1, 1)])
-        second_level(1, 1)
-        finish(0)
-        quantize_rows("a1", slice(4, 5), [("child", 1, 0)])
-        second_level(1, 0)
-        finish(1)
+            (nc.scalar, nc.sync)[s].dma_start(out=out[:, s * P : (s + 1) * P], in_=result[:])

@@ -195,15 +195,18 @@ def tile_picked_yrecnn_gelu_p_kernel(
                 w34_grouped[:, n], raw.rearrange("p j c -> p c j"), 1.0, 0.0, mybir.AluOpType.mult, mybir.AluOpType.add
             )
 
-        e_planes = tile("e_planes", [P, PACK, V], BF16)
+        e_pairs = tile("e_pairs", [P, 2, V, 2], BF16)
         a_planes = tile("a_planes", [P, PACK, V], BF16, tag="right_words")
         for t in range(PACK):
-            nc.vector.tensor_copy(e_planes[:, t], h[t][:].indirect(up2_sb[:]))
+            nc.vector.tensor_copy(e_pairs[:, t // 2, :, t % 2], h[t][:].indirect(up2_sb[:]))
         for t in range(PACK - 1):
             nc.scalar.activation(a_planes[:, t], h[t][:].indirect(up1_sb[:]), COPY)
         nc.vector.tensor_copy(a_planes[:, 3], h[3][:].indirect(up1_sb[:]))
         e_woven = tile("e_woven", [P, V, PACK], BF16)
-        weave(nc.vector.tensor_copy, e_woven[:], e_planes[:])
+        nc.vector.tensor_copy(
+            e_woven[:].rearrange("p v (u e) -> p v u e", e=2).bitcast(I32),
+            e_pairs[:].bitcast(I32).rearrange("p u v e -> p v u e"),
+        )
         quantize("w34", w34_grouped[:].rearrange("p u c j -> p (u c j)"), ["w4", "w3"], tag="h1")
         a_woven = [tile("a_woven%d" % s, [P, P, PACK], BF16) for s in range(2)]
         weave(nc.scalar.copy, a_woven[0][:], a_planes[:, :, :P])

@@ -18,6 +18,7 @@ COPY = mybir.ActivationFunctionType.Copy
 P = 128
 PACK = 4
 HALF = P // 2
+WARM_ROWS = 32
 
 
 def tile_picked_yrecnn_gelu_p_kernel(
@@ -105,21 +106,14 @@ def tile_picked_yrecnn_gelu_p_kernel(
 
         picked_words = [pick_words("left_words", offs_sb)]
         picked_scales = [pick_scales("left_scales", offs_sb)]
-        right_words = tile("right_words", [P, S], U32)
-        picked_words.append(right_words)
-        for n in range(2):
-            nc.vector.tensor_copy(
-                right_words[:, n * V : (n + 1) * V],
-                word_table[:].bitcast(U32).indirect(right_sb[:, 16 * n : 16 * (n + 1)]),
-            )
+        picked_words.append(pick_words("right_words", right_sb))
 
         def picked(u, cols):
             return (picked_words[u][:, cols], picked_scales[u][:, cols])
 
-        warm = psum.tile([P, S], F32, name="warm")
-        for start, width in ((0, 256), (256, 128), (384, 64)):
-            moving = (right_words[:, :width], picked_scales[0][:, :width])
-            mx(warm[:, start : start + width], picked(0, slice(0, P)), moving, True, True)
+        warm = psum.tile([WARM_ROWS, S], F32, name="warm")
+        for n in range(3):
+            mx(warm[:], picked(0, slice(0, WARM_ROWS)), picked(0, slice(0, S)), True, True)
 
         early = [tile("early%d" % u, [P, 2, P, PACK], BF16) for u in range(2)]
         late = tile("late", [P, 2, 2, P, PACK], BF16)

@@ -18,6 +18,7 @@ COPY = mybir.ActivationFunctionType.Copy
 P = 128
 PACK = 4
 HALF = P // 2
+CUT = 256
 WARM_ROWS = 32
 
 
@@ -76,7 +77,8 @@ def tile_picked_yrecnn_gelu_p_kernel(
         right_sb = load_list("right_sb", right)
         halves = [slice(0, H // 2), slice(H // 2, H)]
         w1_raw = [load_rows("w1_raw%d" % n, w1, cols) for n, cols in enumerate(halves)]
-        w2_raw = [load_rows("w2_raw%d" % n, w2, cols) for n, cols in enumerate(halves)]
+        pieces = [halves, [slice(0, CUT), slice(CUT, H)]]
+        w2_raw = [load_rows("w2_raw%d" % n, w2, cols) for n, cols in enumerate(pieces[1])]
 
         def load_dealt(name, w):
             dst = tile(name, [P, PACK, N], F32)
@@ -115,9 +117,12 @@ def tile_picked_yrecnn_gelu_p_kernel(
         for n in range(3):
             mx(warm[:], picked(0, slice(0, WARM_ROWS)), picked(0, slice(0, S)), True, True)
 
-        early = [tile("early%d" % u, [P, 2, P, PACK], BF16) for u in range(2)]
-        late = tile("late", [P, 2, 2, P, PACK], BF16)
-
+        rounded = tile("rounded", [P, 6, P, PACK], BF16)
+        early = tile("early", [P, 2, P, PACK], BF16)
+        homes = [
+            [rounded[:, 0:3], rounded[:, 1:3], rounded[:, 2:3], rounded[:, 5:6]],
+            [early[:, 0:2], early[:, 1:2], rounded[:, 3:4], rounded[:, 4:5]],
+        ]
 
         spans = [[slice(0, S // 2), slice(S // 2, S)]] + [[slice(0, S)]] * (PACK - 1)
         acc = {}
@@ -137,43 +142,62 @@ def tile_picked_yrecnn_gelu_p_kernel(
             for n, cols in enumerate(spans[t]):
                 nc.scalar.activation(h[t][:, cols], acc[t][n][:], GELU)
 
-        def cast(u, half, planes):
-            dst = early[u][:, planes] if planes.start < 2 else late[:, :, u]
-            raw = (w1_raw, w2_raw)[u][half]
-            if u == 0 and planes.start == 2:
-                nc.gpsimd.tensor_scalar(
-                    dst[:, :, half * HALF : (half + 1) * HALF].rearrange("p t (g i) j -> p g t i j", i=2),
-                    raw[:].rearrange("p j (g t i) -> p g t i j", t=PACK, i=2)[:, :, planes],
-                    1.0,
-                    0.0,
-                    mybir.AluOpType.mult,
-                    mybir.AluOpType.add,
-                )
-                return
+        def views(u, n, planes):
+            cols = pieces[u][n]
+            dst = homes[u][planes.start][:, : planes.stop - planes.start]
+            return dst[:, :, cols.start // PACK : cols.stop // PACK], (w1_raw, w2_raw)[u][n][:]
+
+        def cast(u, n, planes):
+            dst, raw = views(u, n, planes)
             nc.scalar.copy(
-                dst[:, :, half * HALF : (half + 1) * HALF].rearrange("p t (g i) j -> p g j t i", i=2),
-                raw[:].rearrange("p j (g t i) -> p g j t i", t=PACK, i=2)[:, :, :, planes],
+                dst.rearrange("p t (g i) j -> p g j t i", i=2),
+                raw.rearrange("p j (g t i) -> p g j t i", t=PACK, i=2)[:, :, :, planes],
             )
 
-        def cast_matrix(u):
-            for planes in (slice(0, 2), slice(2, 4)):
-                cast(u, 0, planes)
-            for planes in (slice(0, 1), slice(1, 2), slice(2, 4)):
-                cast(u, 1, planes)
+        def cast_on_gpsimd(u, n, planes):
+            dst, raw = views(u, n, planes)
+            nc.gpsimd.tensor_scalar(
+                dst.rearrange("p t (g i) j -> p g t i j", i=2),
+                raw.rearrange("p j (g t i) -> p g t i j", t=PACK, i=2)[:, :, planes],
+                1.0,
+                0.0,
+                mybir.AluOpType.mult,
+                mybir.AluOpType.add,
+            )
 
-        cast_matrix(0)
-        for t in range(2):
-            quantize("w1_%d" % t, early[0][:, t].rearrange("p m j -> p (m j)"), [(t, 0)])
+        cast(0, 0, slice(0, 3))
+        cast_on_gpsimd(0, 0, slice(3, 4))
+        for t in range(3):
+            cast(0, 1, slice(t, t + 1))
+        cast_on_gpsimd(0, 1, slice(3, 4))
+        quantize("w1_0", rounded[:, 0].rearrange("p m j -> p (m j)"), [(0, 0)])
+        first_level(0, 0)
+        quantize("w1_12", rounded[:, 1:3].rearrange("p t m j -> p (t m j)"), [(1, 0), (2, 0)])
+        for t in (1, 2):
             first_level(t, 0)
         picked_scales.append(pick_scales("right_scales", right_sb, tag="w1_raw1"))
-        cast_matrix(1)
-        for t in range(2):
-            quantize("w2_%d" % t, early[1][:, t].rearrange("p m j -> p (m j)"), [(t, 1)])
-            first_level(t, 1)
-        for t in range(2, PACK):
-            quantize("late_%d" % t, late[:, t - 2].rearrange("p u m j -> p (u m j)"), [(t, 0), (t, 1)])
-            first_level(t, 0)
-            first_level(t, 1)
+        cast(1, 0, slice(0, 2))
+        cast(1, 0, slice(2, 3))
+        cast_on_gpsimd(1, 0, slice(3, 4))
+        for t in range(PACK):
+            cast(1, 1, slice(t, t + 1))
+        codes = tile("w2_0_codes", [P, P], U32)
+        scales = tile("w2_0_scales", [P, P], U8)
+        for cols in (slice(0, HALF), slice(HALF, P)):
+            nc.vector.quantize_mx(
+                out=codes[:, cols].bitcast(FP8X4),
+                scales=scales[:, cols],
+                in_=early[:, 0, cols].rearrange("p m j -> p (m j)"),
+            )
+        operands[0, 1] = (codes[:], scales[:])
+        first_level(0, 1)
+        quantize("w2_1", early[:, 1].rearrange("p m j -> p (m j)"), [(1, 1)])
+        first_level(1, 1)
+        quantize("w2_2", rounded[:, 3].rearrange("p m j -> p (m j)"), [(2, 1)])
+        first_level(2, 1)
+        quantize("plane_3", rounded[:, 4:6].rearrange("p t m j -> p (t m j)"), [(3, 1), (3, 0)])
+        first_level(3, 0)
+        first_level(3, 1)
         for t in range(PACK):
             activate(t)
 
@@ -183,7 +207,7 @@ def tile_picked_yrecnn_gelu_p_kernel(
                 planes.rearrange("p t (c i) -> p c t i", i=4),
             )
 
-        w34_grouped = tile("w34_grouped", [P, 2, N, PACK], BF16, tag="late")
+        w34_grouped = tile("w34_grouped", [P, 2, N, PACK], BF16, tag="rounded")
         for n, raw in enumerate((w4_raw, w3_raw)):
             nc.gpsimd.tensor_scalar(
                 w34_grouped[:, n], raw.rearrange("p j c -> p c j"), 1.0, 0.0, mybir.AluOpType.mult, mybir.AluOpType.add
@@ -207,7 +231,7 @@ def tile_picked_yrecnn_gelu_p_kernel(
         weave(nc.vector.tensor_copy, a_woven[1][:], a_planes[:, :, P:])
         acc_out = [psum.tile([N, P], F32, name="acc_out%d" % s) for s in range(2)]
 
-        quantize("e", e_woven[:].rearrange("p v t -> p (v t)"), [("e", 0), ("e", 1)])
+        quantize("e", e_woven[:].rearrange("p v t -> p (v t)"), [("e", 0), ("e", 1)], tag="h2")
         for s in range(2):
             mx(acc_out[s][:], operands["w4"], operands["e", s], True, False)
         for s in (1, 0):

@@ -124,18 +124,18 @@ def tile_picked_yrecnn_gelu_p_kernel(
             [early[:, 0:2], early[:, 1:2], rounded[:, 3:4], rounded[:, 4:5]],
         ]
 
-        spans = [[slice(0, S // 2), slice(S // 2, S)]] + [[slice(0, S)]] * (PACK - 1)
+        spans = [[slice(0, S // 4), slice(S // 4, S // 2), slice(S // 2, S)]] + [[slice(0, S)]] * (PACK - 1)
         acc = {}
         h = []
 
-        def first_level(t, u):
-            if u == 0:
+        def first_level(t, u, opens):
+            if opens:
                 acc[t] = [
                     psum.tile([P, cols.stop - cols.start], F32, name="acc%d_%d" % (t, n))
                     for n, cols in enumerate(spans[t])
                 ]
             for n, cols in enumerate(spans[t]):
-                mx(acc[t][n][:], operands[t, u], picked(u, cols), u == 0, u == 1)
+                mx(acc[t][n][:], operands[t, u], picked(u, cols), opens, not opens)
 
         def activate(t):
             h.append(tile("h%d" % t, [P, S], F32))
@@ -170,11 +170,9 @@ def tile_picked_yrecnn_gelu_p_kernel(
         for t in range(3):
             cast(0, 1, slice(t, t + 1))
         cast_on_gpsimd(0, 1, slice(3, 4))
-        quantize("w1_0", rounded[:, 0].rearrange("p m j -> p (m j)"), [(0, 0)])
-        first_level(0, 0)
-        quantize("w1_12", rounded[:, 1:3].rearrange("p t m j -> p (t m j)"), [(1, 0), (2, 0)])
-        for t in (1, 2):
-            first_level(t, 0)
+        for t in range(2):
+            quantize("w1_%d" % t, rounded[:, t].rearrange("p m j -> p (m j)"), [(t, 0)])
+            first_level(t, 0, True)
         picked_scales.append(pick_scales("right_scales", right_sb, tag="w1_raw1"))
         cast(1, 0, slice(0, 2))
         cast(1, 0, slice(2, 3))
@@ -190,14 +188,16 @@ def tile_picked_yrecnn_gelu_p_kernel(
                 in_=early[:, 0, cols].rearrange("p m j -> p (m j)"),
             )
         operands[0, 1] = (codes[:], scales[:])
-        first_level(0, 1)
+        first_level(0, 1, False)
         quantize("w2_1", early[:, 1].rearrange("p m j -> p (m j)"), [(1, 1)])
-        first_level(1, 1)
+        first_level(1, 1, False)
         quantize("w2_2", rounded[:, 3].rearrange("p m j -> p (m j)"), [(2, 1)])
-        first_level(2, 1)
+        first_level(2, 1, True)
+        quantize("w1_2", rounded[:, 2].rearrange("p m j -> p (m j)"), [(2, 0)], tag="early")
+        first_level(2, 0, False)
         quantize("plane_3", rounded[:, 4:6].rearrange("p t m j -> p (t m j)"), [(3, 1), (3, 0)])
-        first_level(3, 0)
-        first_level(3, 1)
+        first_level(3, 0, True)
+        first_level(3, 1, False)
         for t in range(PACK):
             activate(t)
 
@@ -229,7 +229,7 @@ def tile_picked_yrecnn_gelu_p_kernel(
         a_woven = [tile("a_woven%d" % s, [P, P, PACK], BF16) for s in range(2)]
         weave(nc.scalar.copy, a_woven[0][:], a_planes[:, :, :P])
         weave(nc.vector.tensor_copy, a_woven[1][:], a_planes[:, :, P:])
-        acc_out = [psum.tile([N, P], F32, name="acc_out%d" % s) for s in range(2)]
+        acc_out = [psum.tile([N, P], F32, name="acc_out%d" % s, tag=("warm", "acc_out1")[s]) for s in range(2)]
 
         quantize("e", e_woven[:].rearrange("p v t -> p (v t)"), [("e", 0), ("e", 1)], tag="h2")
         for s in range(2):

@@ -19,7 +19,6 @@ P = 128
 PACK = 4
 HALF = P // 2
 CUT = 256
-WARM_ROWS = 32
 
 
 def tile_picked_yrecnn_gelu_p_kernel(
@@ -112,10 +111,6 @@ def tile_picked_yrecnn_gelu_p_kernel(
 
         def picked(u, cols):
             return (picked_words[u][:, cols], picked_scales[u][:, cols])
-
-        warm = psum.tile([WARM_ROWS, S], F32, name="warm")
-        for n in range(3):
-            mx(warm[:], picked(0, slice(0, WARM_ROWS)), picked(0, slice(0, S)), True, True)
 
         rounded = tile("rounded", [P, 6, P, PACK], BF16)
         early = tile("early", [P, 2, P, PACK], BF16)

@@ -165,9 +165,11 @@ def tile_picked_yrecnn_gelu_p_kernel(
         for t in range(3):
             cast(0, 1, slice(t, t + 1))
         cast_on_gpsimd(0, 1, slice(3, 4))
-        for t in range(2):
-            quantize("w1_%d" % t, rounded[:, t].rearrange("p m j -> p (m j)"), [(t, 0)])
-            first_level(t, 0, True)
+        quantize("w1_0", rounded[:, 0].rearrange("p m j -> p (m j)"), [(0, 0)])
+        first_level(0, 0, True)
+        quantize("w1_12", rounded[:, 1:3].rearrange("p t m j -> p (t m j)"), [(1, 0), (2, 0)])
+        first_level(1, 0, True)
+        first_level(2, 0, True)
         picked_scales.append(pick_scales("right_scales", right_sb, tag="w1_raw1"))
         cast(1, 0, slice(0, 2))
         cast(1, 0, slice(2, 3))
@@ -187,9 +189,7 @@ def tile_picked_yrecnn_gelu_p_kernel(
         quantize("w2_1", early[:, 1].rearrange("p m j -> p (m j)"), [(1, 1)])
         first_level(1, 1, False)
         quantize("w2_2", rounded[:, 3].rearrange("p m j -> p (m j)"), [(2, 1)])
-        first_level(2, 1, True)
-        quantize("w1_2", rounded[:, 2].rearrange("p m j -> p (m j)"), [(2, 0)], tag="early")
-        first_level(2, 0, False)
+        first_level(2, 1, False)
         quantize("plane_3", rounded[:, 4:6].rearrange("p t m j -> p (t m j)"), [(3, 1), (3, 0)])
         first_level(3, 0, True)
         first_level(3, 1, False)

from contextlib import ExitStack

import concourse.mybir as mybir

K, T, S, V, H, N = 512, 1024, 512, 256, 512, 128
FLOPS = 2 * (2 * K * H * S + 2 * H * N * V)

F32 = mybir.dt.float32
BF16 = mybir.dt.bfloat16
I32 = mybir.dt.int32
U32 = mybir.dt.uint32
U16 = mybir.dt.uint16
U8 = mybir.dt.uint8
FP8X4 = mybir.dt.float8_e4m3fn_x4
GELU = mybir.ActivationFunctionType.Gelu_apprx_tanh
COPY = mybir.ActivationFunctionType.Copy

P = 128
PACK = 4
HALF = P // 2
CUT = 256


def tile_picked_yrecnn_gelu_p_kernel(
    tc, x_words, x_scales, w1, w2, w3, w4, offs, right, up1, up2, out
):
    nc = tc.nc
    with ExitStack() as ctx:
        lists = ctx.enter_context(tc.tile_pool(name="lists", bufs=1))
        sb = ctx.enter_context(tc.tile_pool(name="sb", bufs=1))
        psum = ctx.enter_context(tc.psum_pool(name="psum", bufs=1))

        def tile(name, shape, dtype, tag=""):
            return sb.tile(shape, dtype, name=name, tag=tag or name, align_bytes=64)

        def load_list(name, src):
            dst = lists.tile(list(src.shape), U16, name=name)
            nc.sync.dma_start(dst[:], src)
            return dst

        def load_rows(name, w, cols):
            dst = tile(name, [P, PACK, cols.stop - cols.start], F32)
            nc.sync.dma_start(out=dst[:], in_=w.rearrange("(p j) c -> p j c", j=PACK)[:, :, cols])
            return dst

        operands = {}

        def quantize(name, src, keys, tag=""):
            codes = tile(name + "_codes", [P, len(keys) * P], U32, tag=tag)
            scales = tile(name + "_scales", [P, len(keys) * P], U8)
            nc.vector.quantize_mx(out=codes[:].bitcast(FP8X4), scales=scales[:], in_=src)
            for n, key in enumerate(keys):
                operands[key] = (codes[:, n * P : (n + 1) * P], scales[:, n * P : (n + 1) * P])

        def mx(acc, stationary, moving, start, stop):
            nc.tensor.matmul_mx(
                out=acc,
                lhsT=stationary[0].bitcast(FP8X4),
                lhsT_scale=stationary[1],
                rhs=moving[0].bitcast(FP8X4),
                rhs_scale=moving[1],
                start=start,
                stop=stop,
            )

        offs_sb = load_list("offs_sb", offs)
        word_table = tile("word_table", [P, T], I32)
        nc.sync.dma_start(out=word_table[:], in_=x_words[0].rearrange("p n r -> p (n r)").bitcast(I32))
        scale_table = tile("scale_table", [P, T], U8)
        nc.vector.memset(scale_table[:].bitcast(I32), 0)
        for q in range(4):
            nc.sync.dma_start(
                out=scale_table[32 * q : 32 * q + 4, :].bitcast(I32),
                in_=x_scales[0, 4 * q : 4 * q + 4, :].bitcast(I32),
            )
        right_sb = load_list("right_sb", right)
        halves = [slice(0, H // 2), slice(H // 2, H)]
        w1_raw = [load_rows("w1_raw%d" % n, w1, cols) for n, cols in enumerate(halves)]
        pieces = [halves, [slice(0, CUT), slice(CUT, H)]]
        w2_raw = [load_rows("w2_raw%d" % n, w2, cols) for n, cols in enumerate(pieces[1])]

        def load_dealt(name, w):
            dst = tile(name, [P, PACK, N], F32)
            for i in range(2):
                nc.sync.dma_start(out=dst[i:P:2], in_=w.rearrange("(g t i) c -> i g t c", t=PACK, i=2)[i])
            return dst[:]

        w4_raw = load_dealt("w4_raw", w4)
        w3_raw = load_dealt("w3_raw", w3)
        up2_sb = load_list("up2_sb", up2)
        up1_sb = load_list("up1_sb", up1)

        warm_in = tile("warm_in", [P, 8], F32)
        warm_out = tile("warm_out", [P, 8], F32)
        nc.vector.memset(warm_in[:], 0.0)
        nc.scalar.activation(warm_out[:], warm_in[:], GELU)

        def pick_words(name, lst):
            words = tile(name, [P, S], U32)
            nc.vector.tensor_copy(words[:], word_table[:].bitcast(U32).indirect(lst[:]))
            return words

        def pick_scales(name, lst, tag=""):
            sc = tile(name, [P, S], U8, tag=tag)
            nc.vector.tensor_copy(sc[:], scale_table[:].indirect(lst[:]))
            return sc

        picked_words = [pick_words("left_words", offs_sb)]
        picked_scales = [pick_scales("left_scales", offs_sb)]
        picked_words.append(pick_words("right_words", right_sb))

        def picked(u, cols):
            return (picked_words[u][:, cols], picked_scales[u][:, cols])

        rounded = tile("rounded", [P, 6, P, PACK], BF16)
        early = tile("early", [P, 2, P, PACK], BF16)
        homes = [
            [rounded[:, 0:3], rounded[:, 1:3], rounded[:, 2:3], rounded[:, 5:6]],
            [early[:, 0:2], early[:, 1:2], rounded[:, 3:4], rounded[:, 4:5]],
        ]

        spans = [[slice(0, S // 4), slice(S // 4, S // 2), slice(S // 2, S)]] + [[slice(0, S)]] * (PACK - 1)
        acc = {}
        h = []

        def first_level(t, u, opens):
            if opens:
                acc[t] = [
                    psum.tile([P, cols.stop - cols.start], F32, name="acc%d_%d" % (t, n))
                    for n, cols in enumerate(spans[t])
                ]
            for n, cols in enumerate(spans[t]):
                mx(acc[t][n][:], operands[t, u], picked(u, cols), opens, not opens)

        def activate(t):
            h.append(tile("h%d" % t, [P, S], F32))
            for n, cols in enumerate(spans[t]):
                nc.scalar.activation(h[t][:, cols], acc[t][n][:], GELU)

        def views(u, n, planes):
            cols = pieces[u][n]
            dst = homes[u][planes.start][:, : planes.stop - planes.start]
            return dst[:, :, cols.start // PACK : cols.stop // PACK], (w1_raw, w2_raw)[u][n][:]

        def cast(u, n, planes):
            dst, raw = views(u, n, planes)
            nc.scalar.copy(
                dst.rearrange("p t (g i) j -> p g j t i", i=2),
                raw.rearrange("p j (g t i) -> p g j t i", t=PACK, i=2)[:, :, :, planes],
            )

        def cast_on_gpsimd(u, n, planes):
            dst, raw = views(u, n, planes)
            nc.gpsimd.tensor_scalar(
                dst.rearrange("p t (g i) j -> p g t i j", i=2),
                raw.rearrange("p j (g t i) -> p g t i j", t=PACK, i=2)[:, :, planes],
                1.0,
                0.0,
                mybir.AluOpType.mult,
                mybir.AluOpType.add,
            )

        cast(0, 0, slice(0, 3))
        cast_on_gpsimd(0, 0, slice(3, 4))
        for t in range(3):
            cast(0, 1, slice(t, t + 1))
        cast_on_gpsimd(0, 1, slice(3, 4))
        quantize("w1_0", rounded[:, 0].rearrange("p m j -> p (m j)"), [(0, 0)])
        first_level(0, 0, True)
        quantize("w1_12", rounded[:, 1:3].rearrange("p t m j -> p (t m j)"), [(1, 0), (2, 0)])
        first_level(1, 0, True)
        first_level(2, 0, True)
        picked_scales.append(pick_scales("right_scales", right_sb, tag="w1_raw1"))
        cast(1, 0, slice(0, 2))
        cast(1, 0, slice(2, 3))
        cast_on_gpsimd(1, 0, slice(3, 4))
        for t in range(PACK):
            cast(1, 1, slice(t, t + 1))
        codes = tile("w2_0_codes", [P, P], U32)
        scales = tile("w2_0_scales", [P, P], U8)
        for cols in (slice(0, HALF), slice(HALF, P)):
            nc.vector.quantize_mx(
                out=codes[:, cols].bitcast(FP8X4),
                scales=scales[:, cols],
                in_=early[:, 0, cols].rearrange("p m j -> p (m j)"),
            )
        operands[0, 1] = (codes[:], scales[:])
        first_level(0, 1, False)
        quantize("w2_1", early[:, 1].rearrange("p m j -> p (m j)"), [(1, 1)])
        first_level(1, 1, False)
        quantize("w2_2", rounded[:, 3].rearrange("p m j -> p (m j)"), [(2, 1)])
        first_level(2, 1, False)
        quantize("plane_3", rounded[:, 4:6].rearrange("p t m j -> p (t m j)"), [(3, 1), (3, 0)])
        first_level(3, 0, True)
        first_level(3, 1, False)
        for t in range(PACK):
            activate(t)

        def weave(engine_copy, dst, planes):
            engine_copy(
                dst.rearrange("p (c i) t -> p c t i", i=4),
                planes.rearrange("p t (c i) -> p c t i", i=4),
            )

        w34_grouped = tile("w34_grouped", [P, 2, N, PACK], BF16, tag="rounded")
        for n, raw in enumerate((w4_raw, w3_raw)):
            nc.gpsimd.tensor_scalar(
                w34_grouped[:, n], raw.rearrange("p j c -> p c j"), 1.0, 0.0, mybir.AluOpType.mult, mybir.AluOpType.add
            )

        e_pairs = tile("e_pairs", [P, 2, V, 2], BF16)
        a_planes = tile("a_planes", [P, PACK, V], BF16, tag="right_words")
        for t in range(PACK):
            nc.vector.tensor_copy(e_pairs[:, t // 2, :, t % 2], h[t][:].indirect(up2_sb[:]))
        for t in range(PACK - 1):
            nc.scalar.activation(a_planes[:, t], h[t][:].indirect(up1_sb[:]), COPY)
        nc.vector.tensor_copy(a_planes[:, 3], h[3][:].indirect(up1_sb[:]))
        e_woven = tile("e_woven", [P, V, PACK], BF16)
        nc.vector.tensor_copy(
            e_woven[:].rearrange("p v (u e) -> p v u e", e=2).bitcast(I32),
            e_pairs[:].bitcast(I32).rearrange("p u v e -> p v u e"),
        )
        quantize("w34", w34_grouped[:].rearrange("p u c j -> p (u c j)"), ["w4", "w3"], tag="h1")
        a_woven = [tile("a_woven%d" % s, [P, P, PACK], BF16) for s in range(2)]
        weave(nc.scalar.copy, a_woven[0][:], a_planes[:, :, :P])
        weave(nc.vector.tensor_copy, a_woven[1][:], a_planes[:, :, P:])
        acc_out = [psum.tile([N, P], F32, name="acc_out%d" % s, tag=("warm", "acc_out1")[s]) for s in range(2)]

        quantize("e", e_woven[:].rearrange("p v t -> p (v t)"), [("e", 0), ("e", 1)], tag="h2")
        for s in range(2):
            mx(acc_out[s][:], operands["w4"], operands["e", s], True, False)
        for s in (1, 0):
            quantize("a%d" % s, a_woven[s][:].rearrange("p v t -> p (v t)"), [("a", s)])
            mx(acc_out[s][:], operands["w3"], operands["a", s], False, True)
            result = tile("result%d" % s, [N, P], F32)
            nc.scalar.activation(result[:], acc_out[s][:], GELU)
            (nc.scalar, nc.sync)[s].dma_start(out=out[:, s * P : (s + 1) * P], in_=result[:])
